import numpy as np, ml_dtypes
CORES = [2,6,10,14,18,22,26,30]
N = 8
BF = ml_dtypes.bfloat16
def gentries(a):
    return np.ascontiguousarray(a.reshape(8, 16, -1).transpose(0, 2, 1)).reshape(8, -1)
def gtable(e):
    e = np.asarray(e); return np.ascontiguousarray(e.reshape(8, -1, 16).transpose(0, 2, 1)).reshape(128, -1).astype(np.int32)
V, B, S, RO = 768, 96, 8, 3
E = V + (N - 1) * B
UM, QM, LAM, H, Z = 1023, 1023, 64, 9, 13
def bars(rng):
    p = np.argsort(rng.random((N, 8, 4, V)), axis=-1); inv = np.argsort(p, axis=-1)
    m = rng.random((N, 8, 4, V)) < 0.4; mi = np.take_along_axis(m, inv, -1)
    L = np.concatenate([p, inv], axis=2); M = np.concatenate([m, mi], axis=2)
    L = np.where(M, np.where(rng.random(L.shape) < 0.5, E, rng.integers(V, E, L.shape)), L)
    return np.take_along_axis(L, np.argsort(rng.random(L.shape), axis=2), 2)
def parts(rng):
    d = {}; size = rng.choice(np.array([224, 288, 352, 448]), (N, 8, 1, 1))
    for k in ("ux", "uy"): d[k] = np.rint((2 * rng.random((N, 8, 16, V)) - 1) * size).astype(np.int64)
    d["ld"] = rng.integers(-2047, 2048, (N, 8, 16, V))
    for k in ("px", "py"): d[k] = rng.integers(0, 8, (N, 8, V))
    d["wt"] = (0.5 + rng.random((N, 8, 16, V))).astype(np.float32)
    d["nb"] = bars(rng); d["bord"] = np.ascontiguousarray(np.argsort(rng.random((N, 8, V)), axis=-1)[..., :B])
    return d
def pack(d):
    out = {}
    for k in ("ux", "uy", "ld"): out[k] = np.ascontiguousarray(d[k].reshape(N, 128, V)).astype(np.int32)
    for k in ("px", "py"): out[k] = np.ascontiguousarray(d[k]).astype(np.int32)
    out["wt"] = np.ascontiguousarray(d["wt"].reshape(N, 128, V)).astype(np.float32)
    out["nb"] = np.stack([gtable(m.reshape(8, 8 * V)) for m in d["nb"]]); out["bord"] = np.stack([gtable(m) for m in d["bord"]])
    return out
def setup_inputs(rng):
    return pack(parts(rng))
def setup_inputs_spread(rng):
    d = parts(rng)
    for k in ("ux", "uy"): d[k] = np.rint((2 * rng.random((N, 8, 16, V)) - 1) * 1023 * np.exp2(-rng.integers(0, 5, (N, 8, 1, V)))).astype(np.int64)
    d["ld"] = np.rint((2 * rng.random((N, 8, 16, V)) - 1) * 2047 * np.exp2(-rng.integers(0, 6, (N, 8, 1, V)))).astype(np.int64)
    d["wt"] = (d["wt"] * np.exp2(rng.integers(-1, 2, (N, 8, 1, V)))).astype(np.float32)
    return pack(d)
def setup_inputs_ends(rng):
    d = parts(rng)
    h = rng.random(d["wt"].shape)
    d["wt"] = np.where(h < 0.4, 4.0, np.where(h < 0.8, 0.25, d["wt"])).astype(np.float32)
    for k, m in (("ux", 1023), ("uy", 1023), ("ld", 2047)):
        x = 2 * rng.integers(0, 2, (N, 8, 16, V)) - 1
        x = np.where(rng.random((N, 8, 1, V)) < 0.6, x[:, :, :1], x)
        one = (np.arange(16)[:, None] == rng.integers(0, 16, (N, 8, 1, V))) & (rng.random((N, 8, 1, V)) < 0.3)
        d[k] = m * np.where(one, -x, x)
    for k in ("px", "py"): d[k] = 7 * rng.integers(0, 2, (N, 8, V))
    h = rng.random((N, 8, 3, V)); x = rng.integers(0, V, (N, 8, 3, V))
    x = np.where(h < 0.15, V - 1, np.where(h > 0.95, E - 1, np.where(h > 0.8, rng.integers(V, E, x.shape), x)))
    L = np.concatenate([np.full((N, 8, 2, V), E), np.zeros((N, 8, 3, V), np.int64), x], axis=2)
    L = np.take_along_axis(L, np.argsort(rng.random(L.shape), axis=2), 2); d["nb"] = L
    d["bord"] = np.where(rng.random((N, 8, B)) < 0.66, (V - 1) * rng.integers(0, 2, (N, 8, B)), d["bord"])
    for r in range(N):
        for g in range(8):
            o = 1 + rng.permutation(V // S - 3)
            for s, v in ((1, V - 1), (-1, V - 1 - S)):
                i, o = o[:12], o[12:]
                c = i[:6] * S + np.arange(6) % (S - 1); n = i[6:] * S + np.arange(6) % (S - 1); far = np.concatenate([n, c])
                for k in ("px", "py"): d[k][r, g, far] = 0; d[k][r, g, v] = 7; d[k][r, g, v - 1] = 7
                for k in ("ux", "uy"):
                    w = d[k][r, g]; w[:, far] = -1023 * s; w[:, v] = 1023 * s; w[:, v - 1] = 1023 * s
                L[r, g, :2, v] = E; L[r, g, 2:, v] = n; L[r, g, :, v - 1] = far[:8]
                for j in range(6): L[r, g, 2 + j, n[j]] = c[j]
    return pack(d)
def setup_inputs_corners(rng):
    d = parts(rng); L = d["nb"]; c = rng.choice(7, (N, 8, 1, V), p=[0.4, 0.1, 0.2, 0.1, 0.1, 0.05, 0.05])
    own = rng.integers(0, V, L.shape); gh = rng.integers(V, E, L.shape); slot = np.arange(8)[:, None]
    L = np.where(c == 1, E, np.where(c == 2, own, L)); L = np.where(c == 3, np.where(slot == (own[:, :, :1] & 7), E, gh), L)
    L = np.where(c == 4, np.where(slot == 7, E, own[:, :, :1]), np.where(c == 5, np.where(slot == 7, own, E), L))
    x = rng.choice(np.array([0, V - 1, V, E - 1, -1]), L.shape)
    d["nb"] = np.where(c == 6, np.where(x < 0, np.arange(V), x), L)
    for r in range(N):
        o = rng.permutation(np.array([4, 6, 7])); lo = V + B * int(rng.integers(0, N - 1))
        d["nb"][r, int(o[0])] = rng.integers(lo, lo + B, (8, V)); d["nb"][r, int(o[1])] = rng.integers(0, V, (8, V))
    for g, m in ((0, 3), (1, 4), (2, 8), (3, 9)):
        o = rng.permutation(16); on = (1 + (o < m).astype(np.int64)) * (1 - 2 * (o & 1)); some = rng.random((N, 1, V)) < 0.8
        for k, p in (("ux", "px"), ("uy", "py")): d[k][:, g] = np.where(some, 64 * d[p][:, g][:, None, :] * on[:, None], d[k][:, g])
    d["px"][:, 5] = 3 + (d["px"][:, 5] & 1); d["py"][:, 5] = 4
    d["ux"][:, 5] = 543 * (2 * (d["px"][:, 5] - 3) - 1)[:, None, :] + rng.integers(0, 2, (N, 16, V))
    return pack(d)
def setup_inputs_crowd(rng):
    d = parts(rng)
    for r in range(N):
        for g in (0, 2, 4, 6):
            i = 1 + rng.permutation(V // S - 1)[:2]; h, c = int(i[0]) * S, int(i[1]) * S
            sc = np.full(16, 128)
            if g == 6: sc[15] = 64
            for k, p in (("ux", "px"), ("uy", "py")):
                d[p][r, g] = np.maximum(d[p][r, g], 1); d[p][r, g, c] = 0; d[k][r, g] = sc[:, None] * d[p][r, g]
            L = d["nb"][r, g]; L[L == c] = h; L[0] = h; L[5] = E
            if g == 2:
                x = L[:, :S]; x[x == E] = h
            if g == 4: L[0, :S * int(rng.integers(2, V // S - 2))] = E
            L[:, h] = c; L[:, c] = E
        i = S * np.arange(V // S); o = rng.permutation(S - 1)[:2]
        c = rng.permutation(i + int(o[0])); n = rng.permutation(i + int(o[1])); v = i + S - 1; s = rng.integers(0, 8, V // S)
        for k, p in (("ux", "px"), ("uy", "py")):
            d[p][r, 7] = np.maximum(d[p][r, 7], 1); d[p][r, 7, c] = 0; d[k][r, 7] = 128 * d[p][r, 7]
        L = d["nb"][r, 7]; L[:, v] = E; L[s, v] = n; L[s, n] = c; L[(s + 1) % 8, c] = E
        o = rng.permutation(S - 1)[:3]; a = i + int(o[0]); b = i + int(o[1]); other = i + int(o[2])
        for k, p in (("ux", "px"), ("uy", "py")):
            d[p][r, 5] = np.maximum(d[p][r, 5], 1); d[p][r, 5, b] = 0
            w = 64 * d[p][r, 5]; w[b] = -64; d[k][r, 5] = w
        n = rng.permutation(a); c = rng.permutation(b); L = d["nb"][r, 5]
        L[:, v] = rng.choice(a, (8, V // S)); L[7, v] = n
        if r % 2 == 0: L[0, v] = E
        else: L[0, v[-4:]] = E
        L[:7, a] = rng.choice(other, (7, V // S)); L[7, n] = c; L[0, b] = E
        x = rng.permutation(i); h = V // S // 2; za = x[:h]; zb = x[h:]
        n = np.concatenate([za, zb]); c = np.concatenate([rng.permutation(zb), rng.permutation(za)]); j = rng.integers(0, 8, V // S)
        act = np.concatenate([i + S - 1 - t for t in range(RO)]); sg = 1 - 2 * (rng.permutation(16) & 1)[:, None]
        for k, p, top, pa, pb, ua, ub in (("ux", "px", 3, 5, 5, 322, 321), ("uy", "py", 4, 3, 4, 189, 255)):
            at = int(rng.integers(0, top)); off = rng.integers(-300, 301, (16, 1))
            d[p][r, 3, act] = at; d[p][r, 3, za] = at + pa; d[p][r, 3, zb] = at + pb
            w = d[k][r, 3]; w[:, act] = off; w[:, za] = off + ua * sg; w[:, zb] = off + ub * sg
        w = d["ld"][r, 3]; w[:, act] = 0; w[:, za] = 0; w[:, zb] = 8 * sg
        L = d["nb"][r, 3]; L[:, i] = E; L[:, act] = E; L[j, n] = c
        for t in range(RO):
            x = rng.permutation(V // S); L[(j[x] - t) % 8, i + S - 1 - t] = n[x]
    return pack(d)
def setup_inputs_calm(rng):
    d = parts(rng)
    for g in (1, 4, 6):
        pj = rng.choice(np.array([0.0, 0.1, 0.5, 0.9]), (N, 1, V))
        for k, p in (("ux", "px"), ("uy", "py")):
            d[k][:, g] = 64 * d[p][:, g][:, None, :] + (rng.random((N, 16, V)) < pj) * rng.integers(1, 4, (N, 16, V))
        d["ld"][:, g] = rng.integers(-16, 16, (N, 16, V))
    r = int(rng.integers(0, N)); d["nb"][r, 6] = E; d["ld"][r, 6] = rng.integers(-2047, 2048, (16, V))
    d["wt"] = (d["wt"] * 0.5).astype(np.float32)
    return pack(d)
def check_ranges(d):
    bad = []
    for k, lo, hi in (("ux", -1023, 1023), ("uy", -1023, 1023), ("ld", -2047, 2047), ("px", 0, 7), ("py", 0, 7), ("nb", 0, E), ("bord", 0, V - 1)):
        if np.min(d[k]) < lo or np.max(d[k]) > hi: bad.append("range of " + k)
    w = np.asarray(d["wt"], np.float64)
    if not np.all((w >= 0.25) & (w <= 4)): bad.append("range of wt")
    return bad
def ext(s, bd):
    out = []
    for r in range(N):
        w = [s[r]]
        for d in range(1, N):
            o = (r - d) % N; w.append(np.take_along_axis(s[o], bd[o][:, None, :], 2))
        w.append(np.zeros(s[r].shape[:2] + (1,), s.dtype)); out.append(np.concatenate(w, axis=2))
    return out
def reference(ux, uy, ld, px, py, wt, nb, bord):
    take = np.take_along_axis
    x = ux.astype(np.int32).reshape(N, 8, 16, V); y = uy.astype(np.int32).reshape(N, 8, 16, V); f = ld.astype(np.int32).reshape(N, 8, 16, V)
    P = px.astype(np.int32); Q = py.astype(np.int32)
    L = np.stack([gentries(m) for m in nb]).astype(np.int64).reshape(N, 8, 8, V); bd = np.stack([gentries(m) for m in bord]).astype(np.int64)
    PX = ext(P[:, :, None], bd); PY = ext(Q[:, :, None], bd); WT = ext(wt.astype(np.float64).reshape(N, 8, 16, V), bd)
    q = np.zeros((N, 8, 8, 16, V), np.int32); w = np.zeros((N, 8, 16, V), np.float64)
    for t in range(RO):
        rho = S - 1 - t; U = np.array(L[:, :, :, rho::S])
        own = U < V; near = np.where(own, U, 0)
        c = np.stack([take(L[:, :, (k + t) % 8], near[:, :, k], 2) for k in range(8)], axis=2)
        ok = own & (c < V) & (c % S != rho)
        for j in range(8): ok = ok & (c != U[:, :, j:j + 1])
        c = np.where(ok, c, 0); sc = []
        for k in range(8):
            i = c[:, :, k]; i4 = i[:, :, None]
            dx = (take(P, i, 2) - P[:, :, rho::S])[:, :, None]; dy = (take(Q, i, 2) - Q[:, :, rho::S])[:, :, None]
            e = (take(x, i4, 3) - x[..., rho::S]) * dx + (take(y, i4, 3) - y[..., rho::S]) * dy
            sc.append(np.sum(np.abs(e) > LAM * (dx * dx + dy * dy), axis=2))
        sc = np.where(ok, np.stack(sc, axis=2), 0); best = np.argmax(sc, axis=2)
        named = take(c, best[:, :, None], 2)[:, :, 0]; does = (np.max(sc, axis=2) >= H) & np.any(U == E, axis=2)
        for r in range(N):
            for g in range(8):
                i = np.flatnonzero(does[r, g])
                if i.size == 0: continue
                M = L[r, g]; u, j = np.unique(named[r, g, i], return_index=True); v = rho + S * i[j]
                m = np.any(M[:, u] == E, axis=0); u, v = u[m], v[m]
                if u.size == 0: continue
                su = np.argmax(M[:, u] == E, axis=0); sv = np.argmax(M[:, v] == E, axis=0)
                M[su, u] = v; M[sv, v] = u
        X = ext(x, bd); Y = ext(y, bd); nx = []; ny = []
        for r in range(N):
            sx = np.zeros((8, 16, V), np.int32); sy = np.zeros((8, 16, V), np.int32)
            for k in range(8):
                ix = np.array(L[r, :, k]); i3 = ix[:, None, :]; full = i3 < E
                dx = np.where(full, take(PX[r], i3, 2) - P[r][:, None], 0); dy = np.where(full, take(PY[r], i3, 2) - Q[r][:, None], 0)
                e = (take(X[r], i3, 2) - x[r]) * dx + (take(Y[r], i3, 2) - y[r]) * dy
                T = LAM * (dx * dx + dy * dy); z = q[r, :, k] + e
                z = np.clip(z - np.clip(z, -T, T), -QM, QM)
                stay = np.sum(z == 0, axis=1) < Z
                z = np.where(stay[:, None], z, 0); L[r, :, k] = np.where(stay, ix, E); q[r, :, k] = z
                sx = sx + z * dx; sy = sy + z * dy; w[r] = w[r] + np.abs(z) * take(WT[r], i3, 2)
            nx.append(np.clip(x[r] + ((sx + 16) >> 5), -UM, UM)); ny.append(np.clip(y[r] + ((sy + f[r] + 16) >> 5), -UM, UM))
        x = np.stack(nx); y = np.stack(ny)
    return {"yx": x.reshape(N, 128, V).astype(np.float32), "yy": y.reshape(N, 128, V).astype(np.float32), "yw": w.reshape(N, 128, V).astype(np.float32)}

def check_inputs(d):
    bad = list(check_ranges(d))
    if not bad:
        for name, y in reference(**d).items():
            for q in range(N):
                v = np.abs(np.asarray(y[q], np.float64)); s = np.sqrt(np.mean(v * v))
                if v.max() > 12 * s or s < 2.0 ** 5: bad.append('%s of rank %d is uneven or too small' % (name, q))
    return bad

@@ -1,0 +1,965 @@
+import numpy as np
+from concourse.bass import DstId, RemoteDMATransfer
+from concourse.mybir import dt, AluOpType, AxisListType, ActivationFunctionType
+
+A = AluOpType
+F = ActivationFunctionType
+s_ = np.s_
+V, B, E, NR = 768, 96, 1440, 8
+MG = 12582912.0
+TBW = 16 * 1152
+ND_, NP_, NG_, NA_ = 4, 5, 3, 4
+
+CFG = {"nz_act": (4, 4, 4), "init_v": 4, "init_v2": 1, "on_eng": 2, "gy_v": 0, "resv": 1, "resv2": 0, "nx1": 3, "act_int": 1,
+       "sum": ("abababab", "ababccpp"), "init_g": 0, "zero_g": 1, "ab_dma": (0, 0, 0), "ab_split": 0, "sg": 1, "clip_act": (0, 0, 0), "ct_v": 0, "early": (0.0, 0.0, 0.0), "early_dma": 0.0,
+       "hop": 120.0, "grain": 100.0, "banks": 8, "seed": 0, "iters": 40, "noise": 300.0}
+CFG.update({"resv2": 1, "init_v": 4, "init_v2": 0, "early": (0.0, 3e3, 3e3), "ct_v": 2, "gy_v": 1, "sum": ("abababab", "ababcppp"),
+            "nx1": -1, "zero_g": 0, "ab_split": 1, "clip_act": (0, 2, 2), "noise": 600.0, "ab_dma": (2, 2, 2), "iters": 30, "pre0": 1, "unp_v": 1})
+
+f32, f16, b16, i32, u16 = "float32", "float16", "bfloat16", "int32", "uint16"
+BUF = {
+    "ia": ([4 * V], i32), "ldh": ([V], f16), "bdi": ([8], i32), "bdu": ([8], u16), "WT": ([E], f32),
+    "XY": ([2, E], f32), "H": ([2, V], f16), "PQ": ([E], b16), "msg": ([2, 288], f16),
+    "land0": ([7, 288], f16), "land1": ([7, 192], f16), "land2": ([7, 192], f16),
+    "TB": ([TBW + 960], b16), "Q": ([6144], f16), "MM": ([2, 6144], f16),
+    "Wu": ([4, 384], u16), "Lp": ([784], f32), "Lh": ([V], f16), "DK": ([2 * V], f16),
+    "gx": ([NG_, 2, 384], f16), "ab": ([NA_, 768], f32), "amt": ([ND_, 384], f16),
+    "nz": ([ND_, 384], b16), "PP": ([NP_ * 1152], f32), "ACC": ([2, 1152], f32), "I5": ([128], b16),
+    "BO1": ([128], b16), "c9": ([384], b16), "PQh": ([V], b16),
+    "pc": ([8], i32), "pf": ([16], f32), "io": ([128], f32), "I": ([128], b16), "nI": ([128], b16),
+    "I32": ([128], f32), "BO": ([128], b16), "BOs": ([128], b16), "BO2": ([128], b16), "LOs": ([128], b16),
+    "nLO2": ([128], b16), "R": ([136], b16), "BG": ([8, 144], b16), "KB": ([144], b16),
+    "nSel": ([8, 128], b16), "Sel": ([2, 128], b16), "SPQ": ([128], b16), "BJ": ([8, 128], b16),
+    "IT": ([128], b16), "nD": ([2, 128], b16), "mk": ([24], f32), "KC": ([V], f16),
+    "DUM": ([B], f32), "dm": ([B], f32), "TM": ([6, 16], b16), "sp": ([384], f16), "TR": ([2, 16], f32),
+    "vw": ([3, 48], f32), "vp": ([3, 8], f32),
+    "o1": ([48], u16), "o2": ([48], u16), "o3": ([8], u16), "o4": ([8], u16), "o5": ([40], u16),
+    "Uc": ([48], f16), "G": ([V], f16), "c16": ([48], f16), "e12": ([2, 48], b16), "dv": ([2, 48], f32),
+    "GP": ([V], b16), "CT": ([3, V], b16), "ind": ([V], b16), "ev": ([384], f32), "n16": ([B], f16),
+    "Fb": ([864], b16), "cwf": ([8], f32), "EQ": ([6, 112], b16), "Fc": ([B], b16), "n2": ([B], f16),
+    "t96": ([8, B], f32), "b96": ([4, B], b16), "VAL": ([576], b16),
+    "tw": ([6, 16], f32), "wa": ([3, 192], f16), "NX": ([3, 864], f32),
+}
+ALIAS = {"xi0": ("ia", 0, V), "xi1": ("ia", V, V), "pqi": ("ia", 2 * V, V), "nbi": ("ia", 3 * V, 384), "lri": ("ia", 3 * V + 384, 384),
+         "ldi": ("ia", 0, V), "cb": ("ia", V, V), "m1": ("ia", 2 * V, 384), "m2": ("ia", 3 * V, 288),
+         "em": ("ind", 0, V), "csq": ("ind", 0, V), "eq": ("GP", 0, 384),
+         "lrh": ("G", 0, 384), "w0": ("DK", 0, 384), "w1": ("DK", 384, 384), "w2": ("DK", V, 384),
+         "Dl": ("DK", 0, V), "Lk": ("DK", V, V), "gc2": ("DK", 0, V), "P": ("PP", 0, 1152), "cg": ("PP", V, 128),
+         "cgf": ("PP", V, 256), "sm": ("PP", 1152 + V, B), "EV": ("PP", 2304 + V, B), "wmsg": ("PP", 2304 + V + 2 * B, B),
+         "spf": ("PP", 3456 + V, 384), "EX": ("VAL", 0, 128), "one": ("VAL", 256, 128), "B8": ("VAL", 384, 128),
+         "bi": ("ia", 3 * V + 288, B), "ci": ("ia", 3 * V + 480, 48)}
+SCRATCH = {k: ("sbuf", [128] + v[0], v[1]) for k, v in BUF.items()}
+SCRATCH["PS"] = ("psum", [128, 8, 512], f32)
+SIZE = {f32: 4, i32: 4, f16: 2, b16: 2, u16: 2}
+NDS = 135
+SEMAPHORES = ["v", "a", "p", "gq"] + ["d%d" % n for n in range(NDS)] + ["rx%d" % n for n in range(4)]
+
+
+def r(name, idx):
+    if name in ALIAS:
+        base, off, n = ALIAS[name]
+        if len(idx) == 3:
+            off += idx[1] * n
+        a, b, c = idx[-1].indices(n)
+        return ("s", base, (idx[0], slice(a + off, b + off, c)))
+    return ("s", name, idx)
+
+
+def ind(win, off):
+    return ("i", win, off)
+
+
+def ps(vb, cols, j=None):
+    return ("p", vb, cols, j)
+
+
+def hbm(name, idx):
+    return ("h", name, idx)
+
+
+_IX = {}
+
+
+def spans(ref):
+    name, idx = ref[1], ref[2]
+    key = (name, str(idx))
+    if key not in _IX:
+        shape, ty = BUF[name]
+        sub = idx[1:] if isinstance(idx, tuple) else ()
+        a = np.arange(int(np.prod(shape))).reshape(shape)[sub]
+        a = np.atleast_1d(a)
+        a = a.reshape(1, -1)
+        z = SIZE[ty]
+        _IX[key] = ([(int(x.min()) * z // 16, (int(x.max()) * z + z + 15) // 16) for x in a], int(a.size))
+    return _IX[key]
+
+
+def count(ref, units):
+    if ref[0] == "s":
+        return spans(ref)[1]
+    if ref[0] == "i":
+        return 16 * spans(ref[2])[1]
+    n = len(range(*ref[2].indices(512)))
+    return n * (units[ref[1]]["n"] if ref[3] is None else 1)
+
+
+def wide(ref):
+    if ref[0] == "s":
+        return SIZE[BUF[ref[1]][1]]
+    return 4
+
+
+def graph(cfg):
+    nodes, units, track = [], [], {}
+
+    def unit(n=1, resv=None):
+        units.append({"n": n, "resv": cfg["resv"] if resv is None else resv, "nodes": []})
+        return len(units) - 1
+
+    def add(eng, calls, outs, ins, cost, lat=0.0, kind="c", after=()):
+        me = len(nodes)
+        deps = set(after)
+        acc = []
+        for ref in ins:
+            if ref[0] == "i":
+                acc += [(ref[1], 0), (ref[2], 0)]
+            else:
+                acc.append((ref, 0))
+        for ref in outs:
+            if ref[0] == "i":
+                acc += [(ref[1], 1), (ref[2], 0)]
+            else:
+                acc.append((ref, 1))
+        mine = set()
+        for ref, w in acc:
+            if ref[0] == "h":
+                continue
+            if ref[0] == "p":
+                u = units[ref[1]]
+                mine.add(ref[1])
+                if me not in u["nodes"]:
+                    u["nodes"].append(me)
+                for j in (range(u["n"]) if ref[3] is None else [ref[3]]):
+                    lst = track.setdefault(("p", ref[1], j), [])
+                    for o, ow in lst:
+                        if o != me and (ow or w or nodes[o]["eng"] != eng):
+                            deps.add(o)
+                    if w:
+                        del lst[:]
+                    lst.append((me, w))
+                continue
+            lst = track.setdefault(ref[1], [])
+            for lo, hi in spans(ref)[0]:
+                keep = []
+                for e in lst:
+                    if e[0] < hi and lo < e[1] and e[2] != me:
+                        if w or e[3]:
+                            deps.add(e[2])
+                        if w and lo <= e[0] and e[1] <= hi:
+                            continue
+                    keep.append(e)
+                keep.append((lo, hi, me, w))
+                lst[:] = keep
+        nodes.append({"eng": eng, "calls": calls, "deps": deps, "cost": cost, "lat": lat, "kind": kind, "units": mine,
+                      "early": cfg["early_dma"] if kind != "c" else 0.0})
+        return me
+
+    def vcost(out, ins, per=1.0):
+        n = count(out, units)
+        if out[0] == "i":
+            return 50 + 0.83 * 3.8 * n
+        if any(x[0] == "i" for x in ins):
+            return 50 + 0.83 * 1.56 * n
+        if all(wide(x) == 2 for x in [out] + ins) and len(ins) < 2:
+            per = per * 0.5
+        return 50 + 0.83 * max(64, per * n)
+
+    def ts(out, in0, s1, s2, op0, op1=None):
+        cols = [x for x in (s1, s2) if isinstance(x, tuple)]
+        args = (out, in0, s1, s2, op0) + (() if op1 is None else (op1,))
+        return add("v", [("tensor_scalar", args, {})], [out], [in0] + cols, vcost(out, [in0]))
+
+    def tt(out, in0, in1, op):
+        per = 2.0 if in0[0] != "p" and in1[0] != "p" else 1.0
+        return add("v", [("tensor_tensor", (out, in0, in1, op), {})], [out], [in0, in1], vcost(out, [in0, in1], per))
+
+    def cp(out, in0):
+        return add("v", [("tensor_copy", (out, in0), {})], [out], [in0], vcost(out, [in0]))
+
+    def ms(out, c):
+        return add("v", [("memset", (out, c), {})], [out], [], vcost(out, []))
+
+    def act(out, in0, fn, scale=1.0, bias=0.0):
+        n = count(out, units)
+        return add("a", [("activation", (out, in0, fn), {"bias": bias, "scale": scale})], [out], [in0] + [bias] * isinstance(bias, tuple),
+                   65 + 0.83 * max(64, n * (1.56 if in0[0] == "i" else 1.0)))
+
+    def pe(mms):
+        c = sum(0.42 * max(64, count(m[2], units)) * (4 if wide(m[2]) == 4 else 1) for m in mms)
+        return add("p", [("matmul", m, {}) for m in mms], [m[0] for m in mms], [m[1] for m in mms] + [m[2] for m in mms], c)
+
+    def grp(out, terms, start=True, stop=True):
+        return [(out, w, x, start and j == 0, stop and j == len(terms) - 1) for j, (w, x) in enumerate(terms)]
+
+    def iota(out, pat, base, cm):
+        kw = {} if BUF[out[1]][1] == i32 else {"allow_small_or_imprecise_dtypes": True}
+        return add("gq", [("iota", (out, pat, base, cm), kw)], [out], [], 130 + 1.66 * count(out, units))
+
+    def asel(out, in0, pat, op, base, cm):
+        return add("gq", [("affine_select", (out, in0, pat, op, 0.0, base, cm), {})], [out], [in0], 170 + 1.66 * count(out, units))
+
+    def dma(q, pairs, accum=False):
+        kw = {"accum_op": A.add} if accum else {}
+        by = sum(count(x, units) * wide(x) for o, i in pairs for x in ([o] if o[0] == "s" else [i]))
+        ins = [i for o, i in pairs] + ([o for o, i in pairs] if accum else [])
+        return add(q, [("dma_start", p, kw) for p in pairs], [o for o, i in pairs], ins,
+                   (900 if q == "gq" else 100) * len(pairs), 1700 + by * 0.21 * (2 if accum else 1), "d")
+
+    def exchange(n, src, lands, lat):
+        me = add("gq", [("send", n, src)], [], [src], 1200, 2000, "d")
+        return add(None, n, lands, [], 0, lat, "x", [me])
+
+    I, nI, I32 = r("I", s_[:, :]), r("nI", s_[:, :]), r("I32", s_[:, :])
+    BO, SPQ = r("BO", s_[:, :]), r("SPQ", s_[:, :])
+    BO1, BO2 = r("BO1", s_[:, :]), r("BO2", s_[:, :])
+
+    def whole(n):
+        return r(n, s_[:, :])
+
+    def col(j):
+        return r("pf", s_[:, j:j + 1])
+
+    def bg(k, i):
+        return r("BG", s_[:, k, 15 - i:143 - i])
+
+    def diag(out, src):
+        return pe(grp(out, [(bg(0, i), src(i)) for i in range(16)]))
+
+    dma("sync", [(r("bdi", s_[:, 0:6]), hbm("bord", s_[:, :]))])
+    dma("sync", [(whole("xi0"), hbm("ux", s_[:, :]))])
+    dma("a", [(whole("xi1"), hbm("uy", s_[:, :]))])
+    ms(whole("pqi"), 0)
+    dma("sync", [(r("pqi", s_[0:128:16, :]), hbm("px", s_[:, :])), (r("pqi", s_[1:128:16, :]), hbm("py", s_[:, :]))])
+    for h, q in ((0, "sync"), (1, "a")):
+        dma(q, [(r("lri", s_[(i % 2) * 64:(i % 2) * 64 + 64, (i // 2) * 48:(i // 2) * 48 + 48]), hbm("nb", s_[i:128:16, :]))
+                for i in range(8 * h, 8 * h + 8)])
+    dma("sync", [(whole("nbi"), hbm("nb", s_[:, :]))])
+    dma("sync", [(r("WT", s_[:, 0:V]), hbm("wt", s_[:, :]))])
+
+    bd = r("bdu", s_[:, 0:6])
+    cp(bd, r("bdi", s_[:, 0:6]))
+    for c in range(2):
+        ts(r("msg", s_[:, 0, c * B:c * B + B]), ind(whole("xi%d" % c), bd), 0.0, None, A.add)
+    ts(r("msg", s_[:, 0, 2 * B:3 * B]), ind(whole("pqi"), bd), 0.0, None, A.add)
+    exchange(0, r("msg", s_[:, 0, :]), [r("land0", s_[:, :, :])], cfg.get("xlat0", 9000))
+    act(whole("wmsg"), ind(r("WT", s_[:, 0:V]), bd), F.Identity)
+    exchange(3, whole("wmsg"), [r("WT", s_[:, V:E])], 9000)
+
+    iota(r("pc", s_[:, 0:1]), [[0, 1]], 0, 1)
+    iota(whole("io"), [[1, 128]], 0, 0)
+    iota(r("cg", s_[:, 0, :]), [[16, 8], [0, 16]], 0, 0)
+    iota(r("cg", s_[:, 1, :]), [[8, 16], [0, 8]], 0, 0)
+    for j, m in ((1, 112), (2, 15), (3, 7), (6, 8), (7, 120)):
+        ts(r("pc", s_[:, j:j + 1]), r("pc", s_[:, 0:1]), m, None, A.bitwise_and)
+    ms(r("pc", s_[:, 4:6]), 0)
+    cp(r("pf", s_[:, 0:8]), whole("pc"))
+    ts(col(4), col(6), 0.0, None, A.is_equal)
+    ts(col(5), col(6), 8.0, None, A.is_equal)
+    ts(col(9), col(3), col(4), 2304.0, A.mult, A.mult)
+    io = whole("io")
+    ts(I, io, col(0), None, A.is_equal)
+    ts(nI, io, col(0), -1.0, A.is_equal, A.mult)
+    ts(I32, io, col(0), None, A.is_equal)
+    ts(BO, r("cg", s_[:, 0, :]), col(1), None, A.is_equal)
+    ts(whole("B8"), r("cg", s_[:, 1, :]), col(7), None, A.is_equal)
+    ts(whole("BOs"), BO, 32768.0, None, A.mult)
+    ts(whole("BO2"), BO, 2048.0, None, A.mult)
+    ts(whole("LOs"), BO, col(4), 1048576.0, A.mult, A.mult)
+    ts(whole("nLO2"), BO, col(4), -2048.0, A.mult, A.mult)
+    ts(r("mk", s_[:, 0:16]), r("io", s_[:, 0:16]), col(2), None, A.is_equal)
+    ts(r("mk", s_[:, 16:24]), r("io", s_[:, 0:8]), col(3), None, A.is_equal)
+    for k in range(8):
+        ts(r("nSel", s_[:, k, :]), BO, r("mk", s_[:, k:k + 1]), -1.0, A.mult, A.mult)
+        ts(r("BJ", s_[:, k, :]), whole("B8"), r("mk", s_[:, 16 + k:17 + k]), None, A.mult)
+    for k in range(2):
+        ts(r("Sel", s_[:, k, :]), BO, r("mk", s_[:, k:k + 1]), None, A.mult)
+        ts(r("nD", s_[:, k, :]), nI, col(4 + k), None, A.mult)
+    tt(SPQ, r("Sel", s_[:, 0, :]), r("Sel", s_[:, 1, :]), A.add)
+    ms(whole("R"), 0.0)
+    ts(r("R", s_[:, 7:135:8]), r("BO", s_[:, 0:128:8]), 512.0, None, A.mult)
+    ts(BO1, BO, 1024.0, None, A.mult)
+    ms(r("BG", s_[:, :, :]), 0.0)
+    ts(r("BG", s_[:, :, 15:143:16]), r("nSel", s_[:, :, 0:128:16]), -1.0, None, A.mult)
+    ms(whole("KB"), 0.0)
+    ts(r("KB", s_[:, 15:143:16]), r("BO", s_[:, 0:128:16]), col(9), None, A.mult)
+    ms(whole("one"), 1.0)
+    for h in range(2):
+        asel(r("EX", s_[:, h, :]), whole("one"), [[-8, 8], [0, 2], [-1, 8]], A.is_equal, -64 * h, 1)
+    asel(whole("IT"), BO, [[16, 8], [0, 2], [1, 8]], A.is_ge, -1, -1)
+    tt(whole("IT"), I, whole("IT"), A.subtract)
+    iota(r("NX", s_[:, 1, 0:V]), [[-2048, 8], [0, B]], 7 * 2048 + E, 0)
+    act(whole("KC"), r("NX", s_[:, 1, 0:V]), F.Identity)
+    io96 = r("io", s_[:, 0:B])
+    ts(whole("DUM"), io96, float(2 ** 20 + 8 * 32768 + 16384 + V), None, A.add)
+    ts(whole("dm"), io96, float(V - 2048), None, A.add)
+    iota(r("sm", s_[:, 0, :]), [[0, 6], [1, 16]], 0, 0)
+    ts(r("TM", s_[:, :, :]), r("sm", s_[:, 0, :]), col(2), None, A.is_gt)
+    iota(whole("spf"), [[0, 8], [-16, 48]], E, 0)
+    ts(whole("sp"), whole("spf"), col(2), None, A.subtract)
+    ts(r("sm", s_[:, 1, 0:48]), r("io", s_[:, 0:48]), 16.0, None, A.mult)
+    for j, w in enumerate((TBW, 6144)):
+        ts(r("TR", s_[:, j, 0:12]), r("sm", s_[:, 1, 0:12]), col(2), float(w), A.add, A.add)
+    ts(r("sm", s_[:, 2, 0:6]), r("sm", s_[:, 1, 0:6]), col(2), 8.0, A.add, A.mult)
+    for t in range(3):
+        ts(r("vw", s_[:, t, :]), r("sm", s_[:, 1, 0:48]), col(6), float(7 - t), A.add, A.add)
+        if t < 2:
+            ts(r("EV", s_[:, t, :]), io96, -8.0, float(E - 7 + t), A.mult, A.add)
+            ts(r("vp", s_[:, t, 0:6]), r("sm", s_[:, 2, 0:6]), float(7 - t), None, A.add)
+    ms(r("Lp", s_[:, V:784]), 0.0)
+    ms(r("Fb", s_[:, V:864]), 0.0)
+    ms(r("TB", s_[:, TBW:TBW + 960]), 0.0)
+    ms(r("NX", s_[:, :, V:864]), 0.0)
+    ms(whole("c9"), 0.28125)
+    ts(whole("I5"), I, 32.0, None, A.mult)
+
+    for c in range(2):
+        if cfg["act_int"]:
+            act(r("XY", s_[:, c, 0:V]), whole("xi%d" % c), F.Identity, bias=MG)
+        else:
+            ts(r("XY", s_[:, c, 0:V]), whole("xi%d" % c), MG, None, A.add)
+        act(r("H", s_[:, c, :]), r("XY", s_[:, c, 0:V]), F.Identity, bias=-MG)
+    dma("sync", [(whole("ldi"), hbm("ld", s_[:, :]))])
+    for o, i in ((r("PQ", s_[:, 0:V]), whole("pqi")), (whole("PQh"), whole("pqi")), (whole("ldh"), whole("ldi"))):
+        if cfg["act_int"]:
+            act(o, i, F.Identity)
+        else:
+            cp(o, i)
+
+    def zero(o):
+        if cfg["zero_g"]:
+            iota(o, [[0, count(o, units)]], 0, 0)
+        else:
+            act(o, whole("KC"), F.Identity, scale=0.0)
+    act(r("ACC", s_[:, :, 768:1152]), whole("KC"), F.Identity, scale=0.0)
+    ts(whole("lrh"), whole("lri"), -1.0, float(E), A.mult, A.add)
+    u = unit(2)
+    pe([(ps(u, s_[i:384:16], b), r("EX", s_[:, i % 2, :]), r("lrh", s_[:, (i // 2) * 48 + 24 * b:(i // 2) * 48 + 24 * b + 24]), True, True)
+        for b in range(2) for i in range(16)])
+    act(whole("Lh"), ps(u, s_[0:384]), F.Identity)
+    cp(r("Lp", s_[:, 0:V]), ps(u, s_[0:384]))
+    wa = [whole("w%d" % j) for j in range(3)]
+    if cfg["pre0"]:
+        ts(wa[0], whole("nbi"), float(E), 2048.0, A.is_equal, A.mult)
+        tt(wa[1], wa[0], whole("sp"), A.min)
+        tt(wa[2], whole("nbi"), wa[1], A.subtract)
+        cp(r("Wu", s_[:, 3, :]), wa[2])
+
+    def unpack(t):
+        for c in range(2):
+            if c < cfg["unp_v"]:
+                ts(r("XY", s_[:, c, V:E]), r("land%d" % t, s_[:, :, c * B:c * B + B]), MG, None, A.add)
+            else:
+                act(r("XY", s_[:, c, V:E]), r("land%d" % t, s_[:, :, c * B:c * B + B]), F.Identity, bias=MG)
+        if t == 0:
+            cp(r("PQ", s_[:, V:E]), r("land0", s_[:, :, 2 * B:3 * B]))
+
+    order = [(hv, k) for hv in range(2) for k in range(8)]
+
+    def lst(w, hv, k):
+        return r("Wu", s_[:, w, k * 48 + hv * 24:k * 48 + hv * 24 + 24])
+
+    def tables(w):
+        for n, (hv, k) in enumerate(order):
+            v0, tb, q0 = 384 * hv, (2 * k + hv) * 1152, (2 * k + hv) * 384
+            dd, sq = r("Q", s_[:, q0:q0 + 384]), r("MM", s_[:, 0, q0:q0 + 384])
+            own = r("PQh", s_[:, v0:v0 + 384])
+            if n % 4 < cfg["init_g"]:
+                act(dd, ind(whole("PQ"), lst(w, hv, k)), F.Identity)
+                u0 = ps(unit(), s_[0:384])
+                pe(grp(u0, [(nI, own), (I, dd)]))
+                act(sq, u0, F.Square, scale=8.0)
+                u1, u2 = unit(2), unit()
+                pe([m for c in range(2) for m in grp(ps(u1, s_[0:384], c), [(r("nSel", s_[:, c, :]), own), (r("Sel", s_[:, c, :]), dd)])])
+            else:
+                tt(dd, ind(whole("PQ"), lst(w, hv, k)), own, A.subtract)
+                act(sq, dd, F.Square, scale=8.0)
+                u1, u2 = unit(2), unit()
+                pe([(ps(u1, s_[0:384], c), r("Sel", s_[:, c, :]), dd, True, True) for c in range(2)])
+            pe([(ps(u2, s_[0:384]), SPQ, sq, True, True)])
+            if n % 4 < cfg["init_v2"]:
+                cp(r("TB", s_[:, tb:tb + 768]), ps(u1, s_[0:384]))
+            else:
+                act(r("TB", s_[:, tb:tb + 768]), ps(u1, s_[0:384]), F.Identity)
+            if n % 4 < cfg["init_v"]:
+                cp(r("TB", s_[:, tb + 768:tb + 1152]), ps(u2, s_[0:384]))
+            else:
+                act(r("TB", s_[:, tb + 768:tb + 1152]), ps(u2, s_[0:384]), F.Identity)
+
+    def relist(t, rows):
+        for pc in range(4):
+            u = unit()
+            for k in (2 * pc, 2 * pc + 1):
+                pe(grp(ps(u, s_[(k % 2) * 48:(k % 2) * 48 + 48]), [(bg(k, i), r(rows, s_[:, i:V:16])) for i in range(16)]))
+            c = s_[:, pc * B:pc * B + B]
+            w = [r("wa", s_[:, j, pc % 2 * B:pc % 2 * B + B]) for j in range(3)]
+            act(w[0], ps(u, s_[0:B]), F.Relu, scale=-2048.0, bias=2048.0)
+            tt(w[1], w[0], r("sp", c), A.min)
+            tt(w[2], ps(u, s_[0:B]), w[1], A.add)
+            ts(r("Wu", s_[:, t, pc * B:pc * B + B]), w[2], -1.0, float(E), A.mult, A.add)
+
+    def step1(t):
+        rho = 7 - t
+        xy, hh = "XY", "H"
+
+        def kc(u, k):
+            return ps(u, s_[(k % 4) * B:(k % 4) * B + B], k // 4)
+        act(whole("em"), whole("Lh"), F.Relu, scale=-1.0, bias=1.0)
+        u = unit(2)
+        pe([(ps(u, s_[0:384], b), whole("IT"), r("em", s_[:, 384 * b:384 * b + 384]), True, True) for b in range(2)])
+        act(r("Fb", s_[:, 0:V]), ps(u, s_[0:384]), F.Relu)
+        Fa = r("Fb", s_[:, rho:V:8])
+        u = unit()
+        pe(grp(ps(u, s_[0:48]), [(r("nD", s_[:, h, :]), r("Lh", s_[:, rho + 8 * h:V:16])) for h in range(2)]))
+        ts(whole("o1"), ps(u, s_[0:48]), float(E), float(V), A.add, A.min)
+        ts(whole("Uc"), ps(u, s_[0:48]), float(E), float(V), A.add, A.min)
+        act(whole("G"), ind(r("Lp", s_[:, 0:V + 1]), whole("o1")), F.Identity)
+        u = unit()
+        pe(grp(ps(u, s_[0:48]), [(bg((i % 8 + t) % 8, i), r("G", s_[:, i:V:16])) for i in range(16)]))
+        c16 = whole("c16")
+        act(c16, ps(u, s_[0:48]), F.Identity, scale=-1.0, bias=float(E))
+        ts(r("ci", s_[:, 0, :]), ps(u, s_[0:48]), -1.0, float(E), A.mult, A.add)
+        ts(r("ci", s_[:, 1, :]), r("ci", s_[:, 0, :]), 7, None, A.bitwise_and)
+        ts(r("e12", s_[:, 0, :]), r("ci", s_[:, 1, :]), float(rho), None, A.is_equal)
+        ts(r("e12", s_[:, 1, :]), c16, float(V), None, A.is_ge)
+        tt(r("dv", s_[:, 0, :]), r("vw", s_[:, t, :]), c16, A.subtract)
+        u = unit()
+        pe([m for j in range(8) for m in grp(ps(u, s_[j * 48:j * 48 + 48]), [(r("BJ", s_[:, j, :]), whole("Uc")), (nI, c16)])])
+        ts(whole("eq"), ps(u, s_[0:384]), 0.0, None, A.is_equal)
+        u = unit()
+        pe(grp(ps(u, s_[0:48]), [(I, r("e12", s_[:, j, :])) for j in range(2)] + [(I, r("eq", s_[:, j * 48:j * 48 + 48])) for j in range(8)]))
+        d1 = r("dv", s_[:, 1, :])
+        ts(d1, ps(u, s_[0:48]), 1.0, None, A.min)
+        tt(d1, d1, r("dv", s_[:, 0, :]), A.mult)
+        tt(d1, d1, c16, A.add)
+        cp(whole("o2"), d1)
+        act(whole("GP"), ind(r("PQ", s_[:, 0:V]), whole("o2")), F.Identity)
+        pa = r("PQh", s_[:, rho:V:8])
+        for c, (w, nw) in enumerate(((r("Sel", s_[:, 0, :]), r("nSel", s_[:, 0, :])), (r("Sel", s_[:, 1, :]), r("nSel", s_[:, 1, :])), (I, nI))):
+            u = unit(2)
+            pe([m for k in range(8) for m in grp(kc(u, k), [(w, r("GP", s_[:, k:V:8])), (nw, pa)])])
+            if c < cfg["ct_v"]:
+                cp(r("CT", s_[:, c, :]), ps(u, s_[0:384]))
+            elif c < 2:
+                act(r("CT", s_[:, c, :]), ps(u, s_[0:384]), F.Identity)
+            else:
+                act(whole("csq"), ps(u, s_[0:384]), F.Square, scale=8.0)
+        u = unit(2)
+        pe([(ps(u, s_[0:384], b), SPQ, r("csq", s_[:, 384 * b:384 * b + 384]), True, True) for b in range(2)])
+        act(r("CT", s_[:, 2, :]), ps(u, s_[0:384]), F.Identity)
+        act(r("gc2", s_[:, 0, :]), ind(r(xy, s_[:, 0, 0:V]), whole("o2")), F.Identity, bias=-MG)
+        if cfg["gy_v"]:
+            ts(r("gc2", s_[:, 1, :]), ind(r(xy, s_[:, 1, 0:V]), whole("o2")), -MG, None, A.add)
+        else:
+            act(r("gc2", s_[:, 1, :]), ind(r(xy, s_[:, 1, 0:V]), whole("o2")), F.Identity, bias=-MG)
+        keys = []
+        for b in range(2):
+            hb = s_[384 * b:384 * b + 384]
+            uu = [unit(), unit()]
+            for c in (1, 0):
+                pe([m for k in range(4 * b, 4 * b + 4) for m in grp(ps(uu[c], s_[(k % 4) * B:(k % 4) * B + B]),
+                    [(I, r("gc2", s_[:, c, k:V:8])), (nI, r(hh, s_[:, c, rho:V:8]))])])
+            z = ps(uu[0], s_[0:384])
+            tt(r("cb", s_[:, hb]), ps(uu[1], s_[0:384]), r("CT", s_[:, 1, hb]), A.mult)
+            tt(z, z, r("CT", s_[:, 0, hb]), A.mult)
+            tt(z, z, r("cb", s_[:, hb]), A.add)
+            act(z, z, F.Abs)
+            tt(r("ind", s_[:, hb]), z, r("CT", s_[:, 2, hb]), A.is_gt)
+            u = unit(1, 0)
+            keys.append(ps(u, s_[0:384]))
+            mm = [(keys[b], I, r("KC", s_[:, hb]), True, False)]
+            for k in range(4 * b, 4 * b + 4):
+                o = ps(u, s_[(k % 4) * B:(k % 4) * B + B])
+                mm += [(o, r("nSel", s_[:, (k + t) % 8, :]), r("G", s_[:, k:V:8]), False, False), (o, whole("LOs"), Fa, False, False)]
+            mm.append((keys[b], whole("BOs"), r("ind", s_[:, hb]), False, True))
+            pe(mm)
+            if b == 0:
+                act(whole("ev"), keys[0], F.Identity)
+        tt(whole("m1"), keys[1], whole("ev"), A.max)
+        tt(r("m2", s_[:, 0:192]), r("m1", s_[:, 0:192]), r("m1", s_[:, 192:384]), A.max)
+        tt(r("m2", s_[:, 192:288]), r("m2", s_[:, 0:B]), r("m2", s_[:, B:192]), A.max)
+        tt(r("bi", s_[:, 0, :]), r("m2", s_[:, 192:288]), whole("DUM"), A.max)
+        ts(r("bi", s_[:, 1, :]), r("bi", s_[:, 0, :]), 2047, None, A.bitwise_and)
+        n16 = whole("n16")
+        cp(n16, r("bi", s_[:, 1, :]))
+        u = unit()
+        diag(ps(u, s_[0:6]), lambda i: r("n16", s_[:, i:B:16]))
+        cp(r("cwf", s_[:, 0:6]), ps(u, s_[0:6]))
+        cp(r("o3", s_[:, 0:6]), ps(u, s_[0:6]))
+        act(whole("Fc"), ind(whole("Fb"), r("o3", s_[:, 0:6])), F.Identity)
+        for b in range(6):
+            ts(r("EQ", s_[:, b, 0:B - 16 * b]), r("n16", s_[:, 16 * b:B]), r("cwf", s_[:, b:b + 1]), None, A.is_equal)
+        tt(r("EQ", s_[:, :, 0:16]), r("EQ", s_[:, :, 0:16]), r("TM", s_[:, :, :]), A.mult)
+        u = unit()
+        pe([(ps(u, s_[0:B]), I, n16, True, False), (ps(u, s_[0:B]), whole("nLO2"), whole("Fc"), False, False)]
+           + [(ps(u, s_[16 * b:B]), whole("BO2"), r("EQ", s_[:, b, 0:B - 16 * b]), False, False) for b in range(5, 0, -1)]
+           + [(ps(u, s_[0:B]), whole("BO2"), r("EQ", s_[:, 0, 0:B]), False, True)])
+        n2 = whole("n2")
+        tt(n2, ps(u, s_[0:B]), whole("dm"), A.min)
+        u = unit()
+        diag(ps(u, s_[0:6]), lambda i: r("n2", s_[:, i:B:16]))
+        o4 = r("o4", s_[:, 0:6])
+        ts(o4, ps(u, s_[0:6]), 2048.0, None, A.add)
+        tq = [r("t96", s_[:, j, :]) for j in (0, 1, 2, 3, 4, 5, 6, 7, 0, 1, 2)]
+        bq = [r("b96", s_[:, j, :]) for j in range(4)]
+        sel = [r("Sel", s_[:, c, :]) for c in range(2)]
+        nsel = [r("nSel", s_[:, c, :]) for c in range(2)]
+        if t < 2:
+            enter(t, u, n2, o4, tq, bq, sel, nsel)
+            return
+        for c in range(3):
+            zero(r("NX", s_[:, c, 0:V]))
+        tt(bq[0], ind(r("PQ", s_[:, 0:864]), o4), r("PQh", s_[:, rho:V:8]), A.subtract)
+        act(bq[1], bq[0], F.Square, scale=8.0)
+        u = unit()
+        pq = [ps(u, s_[j * B:j * B + B]) for j in range(4)]
+        pe([(pq[0], sel[0], bq[0], True, True), (pq[1], sel[1], bq[0], True, True), (pq[2], SPQ, bq[1], True, True)]
+           + grp(pq[3], [(nsel[0], bq[1]), (nsel[1], bq[1])]))
+        for c in range(2):
+            act(tq[6 + c], r(xy, s_[:, c, rho:V:8]), F.Identity)
+            tt(tq[c], ind(r(xy, s_[:, c, 0:864]), o4), tq[6 + c], A.subtract)
+            tt(tq[c], tq[c], pq[c], A.mult)
+        tt(tq[0], tq[0], tq[1], A.add)
+        tt(tq[2], tq[0], pq[2], A.min)
+        tt(tq[2], tq[2], pq[3], A.max)
+        tt(tq[0], tq[0], tq[2], A.subtract)
+        ts(tq[0], tq[0], -1023.0, 1023.0, A.max, A.min)
+        ts(bq[2], tq[0], 0.0, None, A.not_equal)
+        ts(bq[3], n2, float(V - 2048), 16.0, A.is_ge, A.mult)
+        u = unit(1, 0)
+        pe(grp(ps(u, s_[0:B]), [(nI, bq[3]), (BO, bq[2])]))
+        ts(tq[3], ps(u, s_[0:B]), 3.5, None, A.is_ge)
+        tt(tq[4], tq[0], tq[3], A.mult)
+        act(tq[5], tq[4], F.Abs)
+        for c in range(2):
+            tt(tq[6 + c], tq[4], pq[c], A.mult)
+            act(r("NX", s_[:, c, rho:V:8]), tq[6 + c], F.Identity)
+            ts(ind(r("NX", s_[:, c, :]), o4), tq[6 + c], -1.0, 0.0, A.mult, A.add)
+        tt(tq[8], ind(r("WT", s_[:, 0:864]), o4), tq[5], A.mult)
+        act(r("NX", s_[:, 2, rho:V:8]), tq[8], F.Identity)
+        tt(ind(r("NX", s_[:, 2, :]), o4), tq[5], r("WT", s_[:, rho:V:8]), A.mult)
+
+    def enter(t, u, n2, o4, tq, bq, sel, nsel):
+        rho = 7 - t
+        nw = r("tw", s_[:, 0, 6:12])
+        nd = r("NX", s_[:, 0, :])
+        patch = t > 0 or cfg["pre0"]
+        if patch:
+            act(nw, ps(u, s_[0:6]), F.Identity, bias=2048.0)
+        zero(r("NX", s_[:, 0, 0:V]))
+        act(tq[0], n2, F.Identity, scale=-1.0, bias=float(E - 2048))
+        ts(tq[1], n2, float(V - 2048), None, A.is_lt)
+        cp(ind(nd, o4), r("EV", s_[:, t, :]))
+        tt(r("NX", s_[:, 0, rho:V:8]), tq[0], tq[1], A.mult)
+        u = unit(2)
+        pe([(ps(u, s_[0:384], b), I, r("Fb", s_[:, 384 * b:384 * b + 384]), True, True) for b in range(2)])
+        tt(ps(u, s_[0:384]), ps(u, s_[0:384]), r("NX", s_[:, 0, 0:V]), A.mult)
+        tt(whole("Lh"), ps(u, s_[0:384]), whole("Lh"), A.add)
+        relist(t, "Lh")
+        if not patch:
+            return
+        tt(bq[0], ind(r("PQ", s_[:, 0:864]), o4), r("PQh", s_[:, rho:V:8]), A.subtract)
+        act(bq[1], bq[0], F.Square, scale=8.0)
+        u = unit()
+        pe([(ps(u, s_[j * B:j * B + B]), w, bq[0], True, True) for j, w in enumerate((sel[0], nsel[0], sel[1], nsel[1]))]
+           + [(ps(u, s_[384:480]), SPQ, bq[1], True, True)])
+        act(r("VAL", s_[:, 0:480]), ps(u, s_[0:480]), F.Identity)
+        act(r("VAL", s_[:, 480:576]), ps(u, s_[384:480]), F.Identity)
+        u = unit()
+        pe(grp(ps(u, s_[0:6]), [(r("KB", s_[:, 15 - i:143 - i]), r("Fb", s_[:, rho + 8 * i:V:128])) for i in range(16)])
+           + grp(ps(u, s_[6:12]), [(r("KB", s_[:, 15 - i:143 - i]), r("Fc", s_[:, i:B:16])) for i in range(16)]))
+        w = [r("tw", s_[:, j, 0:12]) for j in range(6)]
+        act(r("tw", s_[:, 0, 0:6]), r("vp", s_[:, t, 0:6]), F.Identity)
+        for c in range(2):
+            ts(r("tw", s_[:, 1, 6 * c:6 * c + 6]), nw, float(V), 32768.0, A.is_ge, A.mult)
+        ts(w[2], w[0], 384.0, 768.0, A.is_ge, A.mult)
+        tt(w[1], w[1], w[0], A.add)
+        tt(w[3], ps(u, s_[0:12]), w[2], A.add)
+        tt(w[4], w[3], w[1], A.add)
+        tt(w[4], w[4], r("TR", s_[:, 0, 0:12]), A.min)
+        for c in range(3):
+            ts(r("o5", s_[:, 12 * c:12 * c + 12]), w[4], 384.0 * c, None, A.add)
+        cp(ind(whole("TB"), r("o5", s_[:, 0:36])), whole("VAL"))
+
+    def forces(t):
+        xy, hh, ups = "XY", "H", []
+        row, late = None, []
+        for n, (hv, k) in enumerate(order):
+            d, dp, v0, cb = n % ND_, n % NP_, 384 * hv, 2 * k + hv
+            vs = s_[v0:v0 + 384]
+            tb, sl = cb * 1152, s_[cb * 384:cb * 384 + 384]
+            if k == 0:
+                act(r("ACC", s_[:, hv, 0:384]), r(hh, s_[:, 0, vs]), F.Identity, scale=32.0, bias=0.5)
+                o = ps(unit(), s_[0:384])
+                pe(grp(o, [(whole("I5"), r(hh, s_[:, 1, vs])), (I, r("ldh", s_[:, vs]))]))
+                act(r("ACC", s_[:, hv, 384:768]), o, F.Identity, bias=0.5)
+            u = unit(2)
+            dg, da = n % NG_, n % NA_
+            for c in range(2):
+                act(r("gx", s_[:, dg, c, :]), ind(r(xy, s_[:, c, :]), lst(t, hv, k)), F.Identity, bias=-MG)
+                o = ps(unit(), s_[0:384]) if cfg["ab_split"] else ps(u, s_[0:384], c)
+                pe(grp(o, [(nI, r(hh, s_[:, c, vs])), (I, r("gx", s_[:, dg, c, :]))]))
+                if cfg["ab_split"]:
+                    tt(r("ab", s_[:, da, 384 * c:384 * c + 384]), o, r("TB", s_[:, tb + 384 * c:tb + 384 * c + 384]), A.mult)
+            if not cfg["ab_split"]:
+                tt(r("ab", s_[:, da, :]), ps(u, s_[0:384]), r("TB", s_[:, tb:tb + 768]), A.mult)
+            z, sp_, cn = ps(unit(), s_[0:384]), ps(unit(1, 0), s_[0:384]), ps(unit(1, 0), s_[0:384])
+            sg = r("Q", s_[:, sl]) if cfg["sg"] else sp_
+            ea, eb = r("ab", s_[:, da, 0:384]), r("ab", s_[:, da, 384:768])
+            if n % 4 < cfg["ab_dma"][t]:
+                dma("gq", [(ea, eb)], True)
+                pe(grp(z, ([(I, r("Q", s_[:, sl]))] if t else []) + [(I32, ea)]))
+            else:
+                pe(grp(z, ([(I, r("Q", s_[:, sl]))] if t else []) + [(I32, ea), (I32, eb)]))
+            act(sg, z, F.Sign)
+            act(z, z, F.Abs)
+            amt, nz = r("amt", s_[:, d, :]), r("nz", s_[:, d, :])
+            mc = amt
+            tt(amt, z, r("TB", s_[:, tb + 768:tb + 1152]), A.subtract)
+            if (n % 4) < cfg["nz_act"][t]:
+                act(nz, amt, F.Sign, bias=-0.5)
+                pe(grp(cn, [(BO2, whole("c9")), (BO1, nz)]))
+            else:
+                ts(nz, amt, 0.0, 0.21875, A.is_gt, A.subtract)
+                pe([(cn, BO2, nz, True, True)])
+            mm = r("MM", s_[:, t, sl]) if t < 2 else amt
+            tt(mc, cn, amt, A.min)
+            if n % 4 < cfg["clip_act"][t]:
+                act(mc, mc, F.Relu, scale=-1.0, bias=1023.0)
+                act(mm, mc, F.Relu, scale=-1.0, bias=1023.0)
+            else:
+                ts(mm, mc, 0.0, 1023.0, A.max, A.min)
+            if cfg["sg"] == 1:
+                pe([(sp_, I, sg, True, True)])
+                sg = sp_
+            if t < 2:
+                tt(r("Q", s_[:, sl]), sg, mm, A.mult)
+                qp = ps(unit(1, 0), s_[0:384])
+                pe([(qp, I, r("Q", s_[:, sl]), True, True)])
+            else:
+                qp = sp_
+                tt(qp, sg, mm, A.mult)
+            for c in range(2):
+                tt(r("P", s_[:, dp, 384 * c:384 * c + 384]), qp, r("TB", s_[:, tb + 384 * c:tb + 384 * c + 384]), A.mult)
+            w = 768
+            if t == 2:
+                um = ps(unit(1, 0), s_[0:384])
+                pw = r("P", s_[:, dp, 768:1152])
+                act(pw, ind(whole("WT"), lst(1, hv, k)), F.Identity)
+                pe(grp(um, [(I, r("MM", s_[:, 0, sl])), (I, r("MM", s_[:, 1, sl])), (I, mm)]))
+                tt(pw, um, pw, A.mult)
+                w = 1152
+            how = cfg["sum"][hv][k]
+            if how == "p":
+                late.append(dp)
+            elif how == "b":
+                dq = (n - 1) % NP_
+                dma("gq", [(r("P", s_[:, dq, 0:w]), r("P", s_[:, dp, 0:w]))], True)
+                dma("gq", [(r("ACC", s_[:, hv, 0:w]), r("P", s_[:, dq, 0:w]))], True)
+            elif how == "c":
+                dma("gq", [(r("ACC", s_[:, hv, 0:w]), r("P", s_[:, dp, 0:w]))], True)
+            if t == 2 and k == (7 if hv == 0 else cfg["nx1"]):
+                dma("gq", [(r("ACC", s_[:, hv, :]), r("NX", s_[:, :, vs]))], True)
+            if k < 7:
+                continue
+            if t < 2:
+                row = ps(unit(), s_[0:384])
+                terms = [(r("R", s_[:, 7 - j:135 - j]), r("MM", s_[:, t, (2 * j + hv) * 384:(2 * j + hv) * 384 + 384])) for j in range(8)]
+                pe(grp(row, terms[:7], True, False))
+                pe(grp(row, terms[7:], False, True))
+                tt(r("Lp", s_[:, vs]), row, r("Lh", s_[:, vs]), A.min)
+                act(r("Lh", s_[:, vs]), r("Lp", s_[:, vs]), F.Identity)
+            src = [r("ACC", s_[:, hv, 384 * c:384 * c + 384]) for c in range(3)]
+            if late:
+                for c in range(3 if t == 2 else 2):
+                    o = ps(unit(), s_[0:384])
+                    terms = [(I32, r("P", s_[:, x, 384 * c:384 * c + 384])) for x in late]
+                    terms.insert(len(late) - 1, (I32, src[c]))
+                    if cfg["nx1"] < 0 and t == 2:
+                        terms.insert(0, (I32, r("NX", s_[:, c, vs])))
+                    for j, x in enumerate(terms):
+                        pe(grp(o, [x], j == 0, j == len(terms) - 1))
+                    src[c] = o
+                late = []
+            for c in range(2):
+                up = src[c]
+                act(up, src[c], F.Identity, scale=0.03125, bias=MG)
+                if t < 2:
+                    ups.append((c, vs, up))
+                else:
+                    ts(up, up, MG - 1023.0, MG + 1023.0, A.max, A.min)
+                    o = r("ACC", s_[:, hv, 384 * c:384 * c + 384])
+                    act(o, up, F.Identity, bias=-MG)
+                    dma("sync", [(hbm(("yx", "yy")[c], s_[:, vs]), o)])
+            if t == 2:
+                o = r("ACC", s_[:, hv, 768:1152])
+                if src[2][0] == "p":
+                    act(o, src[2], F.Identity)
+                dma("sync", [(hbm("yw", s_[:, vs]), o)])
+        if t < 2:
+            for c, vs, up in ups:
+                ts(r(xy, s_[:, c, vs]), up, MG - 1023.0, MG + 1023.0, A.max, A.min)
+                act(r(hh, s_[:, c, vs]), r(xy, s_[:, c, vs]), F.Identity, bias=-MG)
+            for c in range(2):
+                o, i = r("msg", s_[:, 1 - t, c * B:c * B + B]), ind(r(xy, s_[:, c, 0:V]), bd)
+                if c:
+                    ts(o, i, -MG, None, A.add)
+                else:
+                    act(o, i, F.Identity, bias=-MG)
+            exchange(t + 1, r("msg", s_[:, 1 - t, 0:192]), [r("land%d" % (t + 1), s_[:, :, :])], cfg.get("xlat", 7000))
+
+    unpack(0)
+    if cfg["pre0"]:
+        tables(3)
+    for t in range(3):
+        first = len(nodes)
+        step1(t)
+        for x in nodes[first:]:
+            x["early"] = cfg["early"][t]
+        if t == 0 and not cfg["pre0"]:
+            tables(0)
+        forces(t)
+        if t == 1:
+            relist(2, "Lh")
+        if t < 2:
+            unpack(t + 1)
+    return nodes, units
+
+
+def place(nodes, units, cfg, prio, back=False):
+    n = len(nodes)
+    hop, grain = cfg["hop"], cfg["grain"]
+    pred = [x["pre"] for x in nodes]
+    succ = [x["suc"] for x in nodes]
+    if back:
+        pred, succ = succ, pred
+    left = [len(x) for x in pred]
+    ready = [j for j in range(n) if left[j] == 0]
+    fin, rdy, start = [0.0] * n, [0.0] * n, [0.0] * n
+    free = {}
+    banks = [(0.0, []) for _ in range(cfg["banks"])]
+    idle = list(range(cfg["banks"]))
+    todo = [len(u["nodes"]) for u in units]
+    phys = [None] * len(units)
+    out, extra = [], {}
+    while ready:
+        best = None
+        if not back:
+            wait = [(prio[j], u) for j in ready for u in nodes[j]["units"] if phys[u] is None]
+            first = min(wait)[1] if wait else None
+            since = sorted(banks[b][0] for b in idle)
+            pairs = sorted((max(banks[b][0], banks[b + 1][0]), b) for b in idle if b + 1 in idle)
+        for j in ready:
+            x = nodes[j]
+            st = rdy[j] + (x["lat"] if back else 0.0)
+            if x["eng"]:
+                st = max(st, free.get(x["eng"], 0.0))
+            new = () if back else [u for u in x["units"] if phys[u] is None]
+            if new:
+                need = sum(units[u]["n"] for u in new)
+                keep = max(units[u]["resv"] for u in new)
+                if keep and first not in new:
+                    keep = max(keep, units[first]["n"] + cfg["resv2"])
+                if len(idle) < need + keep or (need == 2 and not pairs):
+                    continue
+                st = max(st, (pairs[0][0] if need == 2 else since[0]) + hop)
+            key = (int(st / grain), prio[j])
+            if best is None or key < best[0]:
+                best = (key, j, st, new)
+        if best is None:
+            return None
+        _, j, st, new = best
+        x = nodes[j]
+        for u in sorted(new):
+            if units[u]["n"] == 2:
+                phys[u] = [pairs[0][1], pairs[0][1] + 1]
+            else:
+                phys[u] = [min(idle, key=lambda b: (max(banks[b][0] + hop, st), (b + 1 in idle) + (b - 1 in idle), banks[b][0]))]
+            for b in phys[u]:
+                idle.remove(b)
+            extra[j] = extra.get(j, []) + [y for b in phys[u] for y in banks[b][1]]
+        start[j] = st
+        free[x["eng"]] = st + x["cost"]
+        fin[j] = st + x["cost"] + (0.0 if back else x["lat"])
+        out.append(j)
+        ready.remove(j)
+        if not back:
+            for u in x["units"]:
+                todo[u] -= 1
+                if todo[u] == 0:
+                    for b in phys[u]:
+                        banks[b] = (max(fin[y] for y in units[u]["nodes"]), units[u]["nodes"])
+                        idle.append(b)
+        for s in succ[j]:
+            same = nodes[s]["eng"] == x["eng"] == "p"
+            rdy[s] = max(rdy[s], fin[j] + (0.0 if same else hop))
+            left[s] -= 1
+            if left[s] == 0:
+                ready.append(s)
+    return {"end": max(fin), "start": start, "fin": fin, "order": out, "phys": phys, "extra": extra}
+
+
+def search(nodes, units, cfg):
+    n = len(nodes)
+    for x in nodes:
+        x["pre"], x["suc"] = sorted(x["deps"]), []
+    for j, x in enumerate(nodes):
+        for d in x["pre"]:
+            nodes[d]["suc"].append(j)
+    rng = np.random.RandomState(cfg["seed"])
+    best, prio = None, [float(-j) for j in range(n)]
+    for it in range(cfg["iters"]):
+        b = place(nodes, units, cfg, prio, True)
+        noise = rng.rand(n) * cfg["noise"] * (it > 0)
+        f = place(nodes, units, cfg, [-b["fin"][j] + noise[j] - nodes[j]["early"] for j in range(n)])
+        if f is not None and (best is None or f["end"] < best["end"]):
+            best = f
+        if best is not None:
+            prio = [-y for y in (f or best)["fin"]]
+    return best
+
+
+def schedule(nodes, units, cfg):
+    best = search(nodes, units, cfg)
+    out, fin, start, phys = best["order"], best["fin"], best["start"], best["phys"]
+    for j, e in best["extra"].items():
+        nodes[j]["deps"] = nodes[j]["deps"] | set(e)
+    cnt, known, clock, prog, nd, seen = {}, {}, {}, [], 0, {}
+    for j in out:
+        x = nodes[j]
+        if x["kind"] == "x":
+            x["sig"] = ("rx%d" % x["calls"], "rx")
+            clock[j] = {}
+            continue
+        q = x["eng"]
+        kn = known.setdefault(q, {})
+        waits = {}
+        for d in sorted(x["deps"], key=lambda y: -fin[y]):
+            if nodes[d]["eng"] == q == "p":
+                continue
+            sem, val = nodes[d]["sig"]
+            num = 1 if isinstance(val, str) else val
+            if kn.get(sem, 0) < num:
+                waits[sem] = val
+                kn[sem] = num
+                seen[sem] = max(seen.get(sem, 0), num)
+                for k2, v2 in clock[d].items():
+                    kn[k2] = max(kn.get(k2, 0), v2)
+        if x["kind"] == "d":
+            send = x["calls"][0][0] == "send"
+            x["sig"] = ("d%d" % nd, "tx" if send else 16 * len(x["calls"]))
+            nd += 1
+        else:
+            cnt[q] = cnt.get(q, 0) + len(x["calls"])
+            x["sig"] = (q, cnt[q])
+        clock[j] = dict(kn)
+        prog.append((q, list(waits.items()), x["calls"], x["sig"][0], x["kind"]))
+    last = {}
+    for x in nodes:
+        sem, val = x["sig"]
+        num = 1 if isinstance(val, str) else val
+        if seen.get(sem, 0) < num and (sem not in last or isinstance(val, str) or last[sem] < val):
+            last[sem] = val
+    return {"prog": prog, "phys": phys, "last": last, "end": max(fin), "start": start, "fin": fin, "nodes": nodes, "order": out}
+
+
+_PLAN = {}
+
+
+def plan():
+    if "p" not in _PLAN:
+        nodes, units = graph(CFG)
+        _PLAN["p"] = schedule(nodes, units, CFG)
+    return _PLAN["p"]
+
+
+def routes(src, cores, topo):
+    off = [c for c in cores if topo.chip(c) != topo.chip(src)]
+    on = [c for c in cores if c != src and topo.chip(c) == topo.chip(src)]
+    out, used = [], set()
+    if off:
+        eng = [e for e in topo.engines(src, off[0]) if all(e in topo.engines(src, c) for c in off)]
+        used = set(eng)
+        out.append((off, eng))
+    if on:
+        eng = [e for e in topo.engines(src, on[0]) if e not in used]
+        out.append((on, eng[:CFG["on_eng"]]))
+    return out
+
+
+def rank_program(g, core, T, topo):
+    rank = T.rank_of(core)
+    if rank is None:
+        return
+    p = plan()
+    cores = list(T.cores)
+    mine = routes(core, cores, topo)
+    tx = sum(len(e) for _, e in mine)
+    rx = sum(len(e) for c in cores if c != core for to, e in routes(c, cores, topo) if core in to)
+    Q = {"v": g.vector, "a": g.scalar, "p": g.tensor, "gq": g, "sync": g.sync}
+
+    def ap(x):
+        if not isinstance(x, tuple):
+            return x
+        if x[0] in "sh":
+            return T[x[1]][x[2]]
+        if x[0] == "i":
+            return ap(x[1]).indirect(ap(x[2]))
+        b = p["phys"][x[1]]
+        if x[3] is not None:
+            return T.PS[:, b[x[3]], x[2]]
+        if len(b) == 1:
+            return T.PS[:, b[0], x[2]]
+        return T.PS[:, b[0]:b[1] + 1:b[1] - b[0], x[2]]
+
+    def val(v):
+        return {"rx": rx, "tx": tx}[v] if isinstance(v, str) else v
+
+    def place(n, dst):
+        d = (cores.index(dst) - rank) % NR - 1
+        return T.WT[:, V + d * B:V + d * B + B] if n == 3 else T["land%d" % n][:, d, :]
+
+    for q, waits, calls, sem, kind in p["prog"]:
+        e = Q[q]
+        for s, v in waits:
+            e.wait_ge(T.sem[s], val(v))
+        for c in calls:
+            if c[0] == "send":
+                trs = []
+                for to, eng in mine:
+                    ids = [DstId(rid=topo.addr(d)[0], pnc=topo.addr(d)[1]) for d in to]
+                    trs.append(RemoteDMATransfer(dst_ids=ids, dma_engine_mask=sum(1 << x for x in eng), remote_sem=T.sem["rx%d" % c[1]],
+                                                 srcs=[ap(c[2])], dsts=[place(c[1], d) for d in to]))
+                g.remote_dma_fused(trs, local_sem=T.sem[sem])
+                continue
+            a = [ap(x) for x in c[1]]
+            if c[0] == "tensor_scalar":
+                ins = e.tensor_scalar(*a)
+            elif c[0] == "tensor_tensor":
+                ins = e.tensor_tensor(*a)
+            elif c[0] == "tensor_copy":
+                ins = e.tensor_copy(*a)
+            elif c[0] == "memset":
+                ins = e.memset(*a)
+            elif c[0] == "activation":
+                ins = e.activation(*a, bias=ap(c[2]["bias"]), scale=c[2]["scale"])
+            elif c[0] == "matmul":
+                ins = e.matmul(*a)
+            elif c[0] == "iota":
+                ins = e.iota(*a, **c[2])
+            elif c[0] == "affine_select":
+                ins = e.affine_select(*a)
+            else:
+                ins = e.dma_start(*a, **c[2])
+            ins.then_inc(T.sem[sem], 16 if kind == "d" else 1)
+    for s, v in p["last"].items():
+        g.wait_ge(T.sem[s], val(v))

@@ -14,7 +14,11 @@ CFG = {"nz_act": (4, 4, 4), "init_v": 4, "init_v2": 1, "on_eng": 2, "gy_v": 0, "
        "sum": ("abababab", "ababccpp"), "init_g": 0, "zero_g": 1, "ab_dma": (0, 0, 0), "ab_split": 0, "sg": 1, "clip_act": (0, 0, 0), "ct_v": 0, "early": (0.0, 0.0, 0.0), "early_dma": 0.0,
        "hop": 120.0, "grain": 100.0, "banks": 8, "seed": 0, "iters": 40, "noise": 300.0}
 CFG.update({"resv2": 1, "init_v": 4, "init_v2": 0, "early": (0.0, 3e3, 3e3), "ct_v": 2, "gy_v": 1, "sum": ("abababab", "ababcppp"),
-            "nx1": -1, "zero_g": 0, "ab_split": 1, "clip_act": (0, 2, 2), "noise": 600.0, "ab_dma": (2, 2, 2), "iters": 30, "pre0": 1, "unp_v": 1})
+            "nx1": -1, "zero_g": 0, "ab_split": 1, "clip_act": (0, 2, 2), "noise": 600.0, "ab_dma": (2, 2, 2), "iters": 30, "pre0": 1, "unp_v": 1,
+            "gam": 1.56, "scat": 3.8, "fac": 1.0, "tpe": 1, "p2": 0, "pool": 3, "slack": 0.0, "part": 1.0,
+            "clip_act": (0, 0, 0), "init_v2": 1, "noise": 300.0, "pre0": 0, "tree": 1, "vlast": 1, "pen": (0, 0, 0)})
+CFG.update({"slack": 1500.0, "vlast": 2, "sg": 0, "ab_dma": (3, 3, 3), "zero_g": 1, "grain": 60.0, "early": (0, 0, 0), "part": 0.5,
+            "sum": ("abababab", "ababpppp"), "iters": 4, "pen": (0, 2, 2), "seed": 9, "grain": 100.0, "gam": 1.8})
 
 f32, f16, b16, i32, u16 = "float32", "float16", "bfloat16", "int32", "uint16"
 BUF = {
@@ -25,7 +29,7 @@ BUF = {
     "Wu": ([4, 384], u16), "Lp": ([784], f32), "Lh": ([V], f16), "DK": ([2 * V], f16),
     "gx": ([NG_, 2, 384], f16), "ab": ([NA_, 768], f32), "amt": ([ND_, 384], f16),
     "nz": ([ND_, 384], b16), "PP": ([NP_ * 1152], f32), "ACC": ([2, 1152], f32), "I5": ([128], b16),
-    "BO1": ([128], b16), "c9": ([384], b16), "PQh": ([V], b16),
+    "BO1": ([128], b16), "c9": ([384], b16), "PQh": ([V], b16), "CT2": ([128], b16),
     "pc": ([8], i32), "pf": ([16], f32), "io": ([128], f32), "I": ([128], b16), "nI": ([128], b16),
     "I32": ([128], f32), "BO": ([128], b16), "BOs": ([128], b16), "BO2": ([128], b16), "LOs": ([128], b16),
     "nLO2": ([128], b16), "R": ([136], b16), "BG": ([8, 144], b16), "KB": ([144], b16),
@@ -46,7 +50,7 @@ ALIAS = {"xi0": ("ia", 0, V), "xi1": ("ia", V, V), "pqi": ("ia", 2 * V, V), "nbi
          "lrh": ("G", 0, 384), "w0": ("DK", 0, 384), "w1": ("DK", 384, 384), "w2": ("DK", V, 384),
          "Dl": ("DK", 0, V), "Lk": ("DK", V, V), "gc2": ("DK", 0, V), "P": ("PP", 0, 1152), "cg": ("PP", V, 128),
          "cgf": ("PP", V, 256), "sm": ("PP", 1152 + V, B), "EV": ("PP", 2304 + V, B), "wmsg": ("PP", 2304 + V + 2 * B, B),
-         "spf": ("PP", 3456 + V, 384), "EX": ("VAL", 0, 128), "one": ("VAL", 256, 128), "B8": ("VAL", 384, 128),
+         "spf": ("PP", 3456 + V, 384), "EX": ("VAL", 0, 128), "one": ("VAL", 256, 128), "B8": ("VAL", 384, 128), "neg": ("CT2", 0, 128),
          "bi": ("ia", 3 * V + 288, B), "ci": ("ia", 3 * V + 480, 48)}
 SCRATCH = {k: ("sbuf", [128] + v[0], v[1]) for k, v in BUF.items()}
 SCRATCH["PS"] = ("psum", [128, 8, 512], f32)
@@ -160,6 +164,8 @@ def graph(cfg):
                     keep.append(e)
                 keep.append((lo, hi, me, w))
                 lst[:] = keep
+        if kind == "c":
+            cost *= cfg["fac"]
         nodes.append({"eng": eng, "calls": calls, "deps": deps, "cost": cost, "lat": lat, "kind": kind, "units": mine,
                       "early": cfg["early_dma"] if kind != "c" else 0.0})
         return me
@@ -167,9 +173,9 @@ def graph(cfg):
     def vcost(out, ins, per=1.0):
         n = count(out, units)
         if out[0] == "i":
-            return 50 + 0.83 * 3.8 * n
+            return 50 + 0.83 * cfg["scat"] * n
         if any(x[0] == "i" for x in ins):
-            return 50 + 0.83 * 1.56 * n
+            return 50 + 0.83 * cfg["gam"] * n
         if all(wide(x) == 2 for x in [out] + ins) and len(ins) < 2:
             per = per * 0.5
         return 50 + 0.83 * max(64, per * n)
@@ -180,7 +186,7 @@ def graph(cfg):
         return add("v", [("tensor_scalar", args, {})], [out], [in0] + cols, vcost(out, [in0]))
 
     def tt(out, in0, in1, op):
-        per = 2.0 if in0[0] != "p" and in1[0] != "p" else 1.0
+        per = 1.0 if "p" in (in0[0], in1[0]) else 2.0
         return add("v", [("tensor_tensor", (out, in0, in1, op), {})], [out], [in0, in1], vcost(out, [in0, in1], per))
 
     def cp(out, in0):
@@ -192,7 +198,7 @@ def graph(cfg):
     def act(out, in0, fn, scale=1.0, bias=0.0):
         n = count(out, units)
         return add("a", [("activation", (out, in0, fn), {"bias": bias, "scale": scale})], [out], [in0] + [bias] * isinstance(bias, tuple),
-                   65 + 0.83 * max(64, n * (1.56 if in0[0] == "i" else 1.0)))
+                   65 + 0.83 * max(64, n * (cfg["gam"] if in0[0] == "i" else 1.0)))
 
     def pe(mms):
         c = sum(0.42 * max(64, count(m[2], units)) * (4 if wide(m[2]) == 4 else 1) for m in mms)
@@ -278,9 +284,18 @@ def graph(cfg):
     ts(whole("nLO2"), BO, col(4), -2048.0, A.mult, A.mult)
     ts(r("mk", s_[:, 0:16]), r("io", s_[:, 0:16]), col(2), None, A.is_equal)
     ts(r("mk", s_[:, 16:24]), r("io", s_[:, 0:8]), col(3), None, A.is_equal)
+    if cfg["pool"]:
+        ms(whole("neg"), -1.0)
+        ms(whole("one"), 1.0)
     for k in range(8):
-        ts(r("nSel", s_[:, k, :]), BO, r("mk", s_[:, k:k + 1]), -1.0, A.mult, A.mult)
-        ts(r("BJ", s_[:, k, :]), whole("B8"), r("mk", s_[:, 16 + k:17 + k]), None, A.mult)
+        if cfg["pool"] & 1:
+            asel(r("nSel", s_[:, k, :]), whole("neg"), [[-16, 8], [0, 16]], A.is_equal, -k, 1)
+        else:
+            ts(r("nSel", s_[:, k, :]), BO, r("mk", s_[:, k:k + 1]), -1.0, A.mult, A.mult)
+        if cfg["pool"] & 2:
+            asel(r("BJ", s_[:, k, :]), whole("one"), [[-8, 16], [0, 8]], A.is_equal, -k, 1)
+        else:
+            ts(r("BJ", s_[:, k, :]), whole("B8"), r("mk", s_[:, 16 + k:17 + k]), None, A.mult)
     for k in range(2):
         ts(r("Sel", s_[:, k, :]), BO, r("mk", s_[:, k:k + 1]), None, A.mult)
         ts(r("nD", s_[:, k, :]), nI, col(4 + k), None, A.mult)
@@ -292,7 +307,8 @@ def graph(cfg):
     ts(r("BG", s_[:, :, 15:143:16]), r("nSel", s_[:, :, 0:128:16]), -1.0, None, A.mult)
     ms(whole("KB"), 0.0)
     ts(r("KB", s_[:, 15:143:16]), r("BO", s_[:, 0:128:16]), col(9), None, A.mult)
-    ms(whole("one"), 1.0)
+    if not cfg["pool"]:
+        ms(whole("one"), 1.0)
     for h in range(2):
         asel(r("EX", s_[:, h, :]), whole("one"), [[-8, 8], [0, 2], [-1, 8]], A.is_equal, -64 * h, 1)
     asel(whole("IT"), BO, [[16, 8], [0, 2], [1, 8]], A.is_ge, -1, -1)
@@ -373,6 +389,8 @@ def graph(cfg):
             v0, tb, q0 = 384 * hv, (2 * k + hv) * 1152, (2 * k + hv) * 384
             dd, sq = r("Q", s_[:, q0:q0 + 384]), r("MM", s_[:, 0, q0:q0 + 384])
             own = r("PQh", s_[:, v0:v0 + 384])
+            if cfg["tpe"]:
+                sq = r("TB", s_[:, tb + 768:tb + 1152])
             if n % 4 < cfg["init_g"]:
                 act(dd, ind(whole("PQ"), lst(w, hv, k)), F.Identity)
                 u0 = ps(unit(), s_[0:384])
@@ -385,11 +403,14 @@ def graph(cfg):
                 act(sq, dd, F.Square, scale=8.0)
                 u1, u2 = unit(2), unit()
                 pe([(ps(u1, s_[0:384], c), r("Sel", s_[:, c, :]), dd, True, True) for c in range(2)])
-            pe([(ps(u2, s_[0:384]), SPQ, sq, True, True)])
+            if not cfg["tpe"]:
+                pe([(ps(u2, s_[0:384]), SPQ, sq, True, True)])
             if n % 4 < cfg["init_v2"]:
                 cp(r("TB", s_[:, tb:tb + 768]), ps(u1, s_[0:384]))
             else:
                 act(r("TB", s_[:, tb:tb + 768]), ps(u1, s_[0:384]), F.Identity)
+            if cfg["tpe"]:
+                continue
             if n % 4 < cfg["init_v"]:
                 cp(r("TB", s_[:, tb + 768:tb + 1152]), ps(u2, s_[0:384]))
             else:
@@ -483,11 +504,20 @@ def graph(cfg):
             mm.append((keys[b], whole("BOs"), r("ind", s_[:, hb]), False, True))
             pe(mm)
             if b == 0:
-                act(whole("ev"), keys[0], F.Identity)
-        tt(whole("m1"), keys[1], whole("ev"), A.max)
-        tt(r("m2", s_[:, 0:192]), r("m1", s_[:, 0:192]), r("m1", s_[:, 192:384]), A.max)
-        tt(r("m2", s_[:, 192:288]), r("m2", s_[:, 0:B]), r("m2", s_[:, B:192]), A.max)
-        tt(r("bi", s_[:, 0, :]), r("m2", s_[:, 192:288]), whole("DUM"), A.max)
+                if not cfg["tree"]:
+                    act(whole("ev"), keys[0], F.Identity)
+                if cfg["tree"]:
+                    for j in range(4):
+                        tt(r("m1", s_[:, j * B:j * B + B]), ps(u, s_[j * B:j * B + B]), r("m1", s_[:, j * B - B:j * B]) if j else whole("DUM"), A.max)
+        if cfg["tree"]:
+            for j in range(4):
+                tt(r("bi", s_[:, 0, :]) if j == 3 else r("m2", s_[:, j * B:j * B + B]), ps(u, s_[j * B:j * B + B]),
+                   r("m2", s_[:, j * B - B:j * B]) if j else r("m1", s_[:, 288:384]), A.max)
+        else:
+            tt(whole("m1"), keys[1], whole("ev"), A.max)
+            tt(r("m2", s_[:, 0:192]), r("m1", s_[:, 0:192]), r("m1", s_[:, 192:384]), A.max)
+            tt(r("m2", s_[:, 192:288]), r("m2", s_[:, 0:B]), r("m2", s_[:, B:192]), A.max)
+            tt(r("bi", s_[:, 0, :]), r("m2", s_[:, 192:288]), whole("DUM"), A.max)
         ts(r("bi", s_[:, 1, :]), r("bi", s_[:, 0, :]), 2047, None, A.bitwise_and)
         n16 = whole("n16")
         cp(n16, r("bi", s_[:, 1, :]))
@@ -571,7 +601,7 @@ def graph(cfg):
         act(bq[1], bq[0], F.Square, scale=8.0)
         u = unit()
         pe([(ps(u, s_[j * B:j * B + B]), w, bq[0], True, True) for j, w in enumerate((sel[0], nsel[0], sel[1], nsel[1]))]
-           + [(ps(u, s_[384:480]), SPQ, bq[1], True, True)])
+           + [(ps(u, s_[384:480]), I if cfg["tpe"] else SPQ, bq[1], True, True)])
         act(r("VAL", s_[:, 0:480]), ps(u, s_[0:480]), F.Identity)
         act(r("VAL", s_[:, 480:576]), ps(u, s_[384:480]), F.Identity)
         u = unit()
@@ -620,20 +650,36 @@ def graph(cfg):
                 pe(grp(z, ([(I, r("Q", s_[:, sl]))] if t else []) + [(I32, ea)]))
             else:
                 pe(grp(z, ([(I, r("Q", s_[:, sl]))] if t else []) + [(I32, ea), (I32, eb)]))
-            act(sg, z, F.Sign)
-            act(z, z, F.Abs)
+            sgn = act(sg, z, F.Sign)
             amt, nz = r("amt", s_[:, d, :]), r("nz", s_[:, d, :])
-            mc = amt
-            tt(amt, z, r("TB", s_[:, tb + 768:tb + 1152]), A.subtract)
+            mc, pen = amt, (n + 2) % 4 < cfg["pen"][t]
+            if cfg["tpe"]:
+                act(eb, z, F.Abs)
+                o = ps(unit(1, 0), s_[0:384])
+                nodes[pe([(o, SPQ, r("TB", s_[:, tb + 768:tb + 1152]), True, True)])]["deps"].add(sgn)
+                tt(amt, eb, o, A.subtract)
+            else:
+                act(z, z, F.Abs)
+                tt(amt, z, r("TB", s_[:, tb + 768:tb + 1152]), A.subtract)
             if (n % 4) < cfg["nz_act"][t]:
                 act(nz, amt, F.Sign, bias=-0.5)
-                pe(grp(cn, [(BO2, whole("c9")), (BO1, nz)]))
+                pe(grp(cn, [(BO2, whole("c9"))] * (not pen) + [(BO1, nz)]))
+                off = 9216.0
             else:
                 ts(nz, amt, 0.0, 0.21875, A.is_gt, A.subtract)
                 pe([(cn, BO2, nz, True, True)])
+                off = 0.0
             mm = r("MM", s_[:, t, sl]) if t < 2 else amt
-            tt(mc, cn, amt, A.min)
-            if n % 4 < cfg["clip_act"][t]:
+            if pen:
+                act(nz, cn, F.Relu, scale=-32.0, bias=-32.0 * off)
+                o = ps(unit(1, 0), s_[0:384])
+                pe(grp(o, [(I, amt), (nI, nz)]))
+                ts(mm, o, 0.0, 1023.0, A.max, A.min)
+            else:
+                tt(mc, cn, amt, A.min)
+            if pen:
+                pass
+            elif n % 4 < cfg["clip_act"][t]:
                 act(mc, mc, F.Relu, scale=-1.0, bias=1023.0)
                 act(mm, mc, F.Relu, scale=-1.0, bias=1023.0)
             else:
@@ -643,12 +689,17 @@ def graph(cfg):
                 sg = sp_
             if t < 2:
                 tt(r("Q", s_[:, sl]), sg, mm, A.mult)
-                qp = ps(unit(1, 0), s_[0:384])
-                pe([(qp, I, r("Q", s_[:, sl]), True, True)])
+                if cfg["p2"]:
+                    u = unit(2, 0)
+                    pe([(ps(u, s_[0:384], c), I, r("Q", s_[:, sl]), True, True) for c in range(2)])
+                    tt(r("P", s_[:, dp, 0:768]), ps(u, s_[0:384]), r("TB", s_[:, tb:tb + 768]), A.mult)
+                else:
+                    qp = ps(unit(1, 0), s_[0:384])
+                    pe([(qp, I, r("Q", s_[:, sl]), True, True)])
             else:
                 qp = sp_
                 tt(qp, sg, mm, A.mult)
-            for c in range(2):
+            for c in range(0 if t < 2 and cfg["p2"] else 2):
                 tt(r("P", s_[:, dp, 384 * c:384 * c + 384]), qp, r("TB", s_[:, tb + 384 * c:tb + 384 * c + 384]), A.mult)
             w = 768
             if t == 2:
@@ -686,8 +737,11 @@ def graph(cfg):
                     terms.insert(len(late) - 1, (I32, src[c]))
                     if cfg["nx1"] < 0 and t == 2:
                         terms.insert(0, (I32, r("NX", s_[:, c, vs])))
-                    for j, x in enumerate(terms):
-                        pe(grp(o, [x], j == 0, j == len(terms) - 1))
+                    nv = cfg["vlast"]
+                    for j, x in enumerate(terms[:len(terms) - nv]):
+                        pe(grp(o, [x], j == 0, j == len(terms) - nv - 1))
+                    for x in terms[len(terms) - nv:]:
+                        tt(o, o, x[1], A.add)
                     src[c] = o
                 late = []
             for c in range(2):
@@ -752,7 +806,7 @@ def place(nodes, units, cfg, prio, back=False):
     phys = [None] * len(units)
     out, extra = [], {}
     while ready:
-        best = None
+        best, can = None, []
         if not back:
             wait = [(prio[j], u) for j in ready for u in nodes[j]["units"] if phys[u] is None]
             first = min(wait)[1] if wait else None
@@ -773,10 +827,16 @@ def place(nodes, units, cfg, prio, back=False):
                     continue
                 st = max(st, (pairs[0][0] if need == 2 else since[0]) + hop)
             key = (int(st / grain), prio[j])
+            can.append((key, j, st, new))
             if best is None or key < best[0]:
-                best = (key, j, st, new)
+                best = can[-1]
         if best is None:
             return None
+        if not back and cfg["slack"]:
+            x = nodes[best[1]]
+            for c in can:
+                if nodes[c[1]]["eng"] == x["eng"] and prio[c[1]] + cfg["slack"] < prio[best[1]] and c[2] < best[2] + x["cost"] * cfg["part"]:
+                    best, x = c, nodes[c[1]]
         _, j, st, new = best
         x = nodes[j]
         for u in sorted(new):

import numpy as np
from concourse.bass import DstId, RemoteDMATransfer
from concourse.mybir import dt, AluOpType, AxisListType, ActivationFunctionType

A = AluOpType
F = ActivationFunctionType
s_ = np.s_
V, B, E, NR = 768, 96, 1440, 8
MG = 12582912.0
TBW = 16 * 1152
ND_, NP_, NG_, NA_ = 4, 5, 3, 4

CFG = {"nz_act": (4, 4, 4), "init_v": 4, "init_v2": 1, "on_eng": 2, "gy_v": 0, "resv": 1, "resv2": 0, "nx1": 3, "act_int": 1,
       "sum": ("abababab", "ababccpp"), "init_g": 0, "zero_g": 1, "ab_dma": (0, 0, 0), "ab_split": 0, "sg": 1, "clip_act": (0, 0, 0), "ct_v": 0, "early": (0.0, 0.0, 0.0), "early_dma": 0.0,
       "hop": 120.0, "grain": 100.0, "banks": 8, "seed": 0, "iters": 40, "noise": 300.0}
CFG.update({"resv2": 1, "init_v": 4, "init_v2": 0, "early": (0.0, 3e3, 3e3), "ct_v": 2, "gy_v": 1, "sum": ("abababab", "ababcppp"),
            "nx1": -1, "zero_g": 0, "ab_split": 1, "clip_act": (0, 2, 2), "noise": 600.0, "ab_dma": (2, 2, 2), "iters": 30, "pre0": 1, "unp_v": 1,
            "gam": 1.56, "scat": 3.8, "fac": 1.0, "tpe": 1, "p2": 0, "pool": 3, "slack": 0.0, "part": 1.0,
            "clip_act": (0, 0, 0), "init_v2": 1, "noise": 300.0, "pre0": 0, "tree": 1, "vlast": 1, "pen": (0, 0, 0)})
CFG.update({"slack": 1500.0, "vlast": 2, "sg": 0, "ab_dma": (3, 3, 3), "zero_g": 1, "grain": 60.0, "early": (0, 0, 0), "part": 0.5,
            "sum": ("abababab", "ababpppp"), "iters": 4, "pen": (0, 2, 2), "seed": 9, "grain": 100.0, "gam": 1.8})

f32, f16, b16, i32, u16 = "float32", "float16", "bfloat16", "int32", "uint16"
BUF = {
    "ia": ([4 * V], i32), "ldh": ([V], f16), "bdi": ([8], i32), "bdu": ([8], u16), "WT": ([E], f32),
    "XY": ([2, E], f32), "H": ([2, V], f16), "PQ": ([E], b16), "msg": ([2, 288], f16),
    "land0": ([7, 288], f16), "land1": ([7, 192], f16), "land2": ([7, 192], f16),
    "TB": ([TBW + 960], b16), "Q": ([6144], f16), "MM": ([2, 6144], f16),
    "Wu": ([4, 384], u16), "Lp": ([784], f32), "Lh": ([V], f16), "DK": ([2 * V], f16),
    "gx": ([NG_, 2, 384], f16), "ab": ([NA_, 768], f32), "amt": ([ND_, 384], f16),
    "nz": ([ND_, 384], b16), "PP": ([NP_ * 1152], f32), "ACC": ([2, 1152], f32), "I5": ([128], b16),
    "BO1": ([128], b16), "c9": ([384], b16), "PQh": ([V], b16), "CT2": ([128], b16),
    "pc": ([8], i32), "pf": ([16], f32), "io": ([128], f32), "I": ([128], b16), "nI": ([128], b16),
    "I32": ([128], f32), "BO": ([128], b16), "BOs": ([128], b16), "BO2": ([128], b16), "LOs": ([128], b16),
    "nLO2": ([128], b16), "R": ([136], b16), "BG": ([8, 144], b16), "KB": ([144], b16),
    "nSel": ([8, 128], b16), "Sel": ([2, 128], b16), "SPQ": ([128], b16), "BJ": ([8, 128], b16),
    "IT": ([128], b16), "nD": ([2, 128], b16), "mk": ([24], f32), "KC": ([V], f16),
    "DUM": ([B], f32), "dm": ([B], f32), "TM": ([6, 16], b16), "sp": ([384], f16), "TR": ([2, 16], f32),
    "vw": ([3, 48], f32), "vp": ([3, 8], f32),
    "o1": ([48], u16), "o2": ([48], u16), "o3": ([8], u16), "o4": ([8], u16), "o5": ([40], u16),
    "Uc": ([48], f16), "G": ([V], f16), "c16": ([48], f16), "e12": ([2, 48], b16), "dv": ([2, 48], f32),
    "GP": ([V], b16), "CT": ([3, V], b16), "ind": ([V], b16), "ev": ([384], f32), "n16": ([B], f16),
    "Fb": ([864], b16), "cwf": ([8], f32), "EQ": ([6, 112], b16), "Fc": ([B], b16), "n2": ([B], f16),
    "t96": ([8, B], f32), "b96": ([4, B], b16), "VAL": ([576], b16),
    "tw": ([6, 16], f32), "wa": ([3, 192], f16), "NX": ([3, 864], f32),
}
ALIAS = {"xi0": ("ia", 0, V), "xi1": ("ia", V, V), "pqi": ("ia", 2 * V, V), "nbi": ("ia", 3 * V, 384), "lri": ("ia", 3 * V + 384, 384),
         "ldi": ("ia", 0, V), "cb": ("ia", V, V), "m1": ("ia", 2 * V, 384), "m2": ("ia", 3 * V, 288),
         "em": ("ind", 0, V), "csq": ("ind", 0, V), "eq": ("GP", 0, 384),
         "lrh": ("G", 0, 384), "w0": ("DK", 0, 384), "w1": ("DK", 384, 384), "w2": ("DK", V, 384),
         "Dl": ("DK", 0, V), "Lk": ("DK", V, V), "gc2": ("DK", 0, V), "P": ("PP", 0, 1152), "cg": ("PP", V, 128),
         "cgf": ("PP", V, 256), "sm": ("PP", 1152 + V, B), "EV": ("PP", 2304 + V, B), "wmsg": ("PP", 2304 + V + 2 * B, B),
         "spf": ("PP", 3456 + V, 384), "EX": ("VAL", 0, 128), "one": ("VAL", 256, 128), "B8": ("VAL", 384, 128), "neg": ("CT2", 0, 128),
         "bi": ("ia", 3 * V + 288, B), "ci": ("ia", 3 * V + 480, 48)}
SCRATCH = {k: ("sbuf", [128] + v[0], v[1]) for k, v in BUF.items()}
SCRATCH["PS"] = ("psum", [128, 8, 512], f32)
SIZE = {f32: 4, i32: 4, f16: 2, b16: 2, u16: 2}
NDS = 135
SEMAPHORES = ["v", "a", "p", "gq"] + ["d%d" % n for n in range(NDS)] + ["rx%d" % n for n in range(4)]


def r(name, idx):
    if name in ALIAS:
        base, off, n = ALIAS[name]
        if len(idx) == 3:
            off += idx[1] * n
        a, b, c = idx[-1].indices(n)
        return ("s", base, (idx[0], slice(a + off, b + off, c)))
    return ("s", name, idx)


def ind(win, off):
    return ("i", win, off)


def ps(vb, cols, j=None):
    return ("p", vb, cols, j)


def hbm(name, idx):
    return ("h", name, idx)


_IX = {}


def spans(ref):
    name, idx = ref[1], ref[2]
    key = (name, str(idx))
    if key not in _IX:
        shape, ty = BUF[name]
        sub = idx[1:] if isinstance(idx, tuple) else ()
        a = np.arange(int(np.prod(shape))).reshape(shape)[sub]
        a = np.atleast_1d(a)
        a = a.reshape(1, -1)
        z = SIZE[ty]
        _IX[key] = ([(int(x.min()) * z // 16, (int(x.max()) * z + z + 15) // 16) for x in a], int(a.size))
    return _IX[key]


def count(ref, units):
    if ref[0] == "s":
        return spans(ref)[1]
    if ref[0] == "i":
        return 16 * spans(ref[2])[1]
    n = len(range(*ref[2].indices(512)))
    return n * (units[ref[1]]["n"] if ref[3] is None else 1)


def wide(ref):
    if ref[0] == "s":
        return SIZE[BUF[ref[1]][1]]
    return 4


def graph(cfg):
    nodes, units, track = [], [], {}

    def unit(n=1, resv=None):
        units.append({"n": n, "resv": cfg["resv"] if resv is None else resv, "nodes": []})
        return len(units) - 1

    def add(eng, calls, outs, ins, cost, lat=0.0, kind="c", after=()):
        me = len(nodes)
        deps = set(after)
        acc = []
        for ref in ins:
            if ref[0] == "i":
                acc += [(ref[1], 0), (ref[2], 0)]
            else:
                acc.append((ref, 0))
        for ref in outs:
            if ref[0] == "i":
                acc += [(ref[1], 1), (ref[2], 0)]
            else:
                acc.append((ref, 1))
        mine = set()
        for ref, w in acc:
            if ref[0] == "h":
                continue
            if ref[0] == "p":
                u = units[ref[1]]
                mine.add(ref[1])
                if me not in u["nodes"]:
                    u["nodes"].append(me)
                for j in (range(u["n"]) if ref[3] is None else [ref[3]]):
                    lst = track.setdefault(("p", ref[1], j), [])
                    for o, ow in lst:
                        if o != me and (ow or w or nodes[o]["eng"] != eng):
                            deps.add(o)
                    if w:
                        del lst[:]
                    lst.append((me, w))
                continue
            lst = track.setdefault(ref[1], [])
            for lo, hi in spans(ref)[0]:
                keep = []
                for e in lst:
                    if e[0] < hi and lo < e[1] and e[2] != me:
                        if w or e[3]:
                            deps.add(e[2])
                        if w and lo <= e[0] and e[1] <= hi:
                            continue
                    keep.append(e)
                keep.append((lo, hi, me, w))
                lst[:] = keep
        if kind == "c":
            cost *= cfg["fac"]
        nodes.append({"eng": eng, "calls": calls, "deps": deps, "cost": cost, "lat": lat, "kind": kind, "units": mine,
                      "early": cfg["early_dma"] if kind != "c" else 0.0})
        return me

    def vcost(out, ins, per=1.0):
        n = count(out, units)
        if out[0] == "i":
            return 50 + 0.83 * cfg["scat"] * n
        if any(x[0] == "i" for x in ins):
            return 50 + 0.83 * cfg["gam"] * n
        if all(wide(x) == 2 for x in [out] + ins) and len(ins) < 2:
            per = per * 0.5
        return 50 + 0.83 * max(64, per * n)

    def ts(out, in0, s1, s2, op0, op1=None):
        cols = [x for x in (s1, s2) if isinstance(x, tuple)]
        args = (out, in0, s1, s2, op0) + (() if op1 is None else (op1,))
        return add("v", [("tensor_scalar", args, {})], [out], [in0] + cols, vcost(out, [in0]))

    def tt(out, in0, in1, op):
        per = 1.0 if "p" in (in0[0], in1[0]) else 2.0
        return add("v", [("tensor_tensor", (out, in0, in1, op), {})], [out], [in0, in1], vcost(out, [in0, in1], per))

    def cp(out, in0):
        return add("v", [("tensor_copy", (out, in0), {})], [out], [in0], vcost(out, [in0]))

    def ms(out, c):
        return add("v", [("memset", (out, c), {})], [out], [], vcost(out, []))

    def act(out, in0, fn, scale=1.0, bias=0.0):
        n = count(out, units)
        return add("a", [("activation", (out, in0, fn), {"bias": bias, "scale": scale})], [out], [in0] + [bias] * isinstance(bias, tuple),
                   65 + 0.83 * max(64, n * (cfg["gam"] if in0[0] == "i" else 1.0)))

    def pe(mms):
        c = sum(0.42 * max(64, count(m[2], units)) * (4 if wide(m[2]) == 4 else 1) for m in mms)
        return add("p", [("matmul", m, {}) for m in mms], [m[0] for m in mms], [m[1] for m in mms] + [m[2] for m in mms], c)

    def grp(out, terms, start=True, stop=True):
        return [(out, w, x, start and j == 0, stop and j == len(terms) - 1) for j, (w, x) in enumerate(terms)]

    def iota(out, pat, base, cm):
        kw = {} if BUF[out[1]][1] == i32 else {"allow_small_or_imprecise_dtypes": True}
        return add("gq", [("iota", (out, pat, base, cm), kw)], [out], [], 130 + 1.66 * count(out, units))

    def asel(out, in0, pat, op, base, cm):
        return add("gq", [("affine_select", (out, in0, pat, op, 0.0, base, cm), {})], [out], [in0], 170 + 1.66 * count(out, units))

    def dma(q, pairs, accum=False):
        kw = {"accum_op": A.add} if accum else {}
        by = sum(count(x, units) * wide(x) for o, i in pairs for x in ([o] if o[0] == "s" else [i]))
        ins = [i for o, i in pairs] + ([o for o, i in pairs] if accum else [])
        return add(q, [("dma_start", p, kw) for p in pairs], [o for o, i in pairs], ins,
                   (900 if q == "gq" else 100) * len(pairs), 1700 + by * 0.21 * (2 if accum else 1), "d")

    def exchange(n, src, lands, lat):
        me = add("gq", [("send", n, src)], [], [src], 1200, 2000, "d")
        return add(None, n, lands, [], 0, lat, "x", [me])

    I, nI, I32 = r("I", s_[:, :]), r("nI", s_[:, :]), r("I32", s_[:, :])
    BO, SPQ = r("BO", s_[:, :]), r("SPQ", s_[:, :])
    BO1, BO2 = r("BO1", s_[:, :]), r("BO2", s_[:, :])

    def whole(n):
        return r(n, s_[:, :])

    def col(j):
        return r("pf", s_[:, j:j + 1])

    def bg(k, i):
        return r("BG", s_[:, k, 15 - i:143 - i])

    def diag(out, src):
        return pe(grp(out, [(bg(0, i), src(i)) for i in range(16)]))

    dma("sync", [(r("bdi", s_[:, 0:6]), hbm("bord", s_[:, :]))])
    dma("sync", [(whole("xi0"), hbm("ux", s_[:, :]))])
    dma("a", [(whole("xi1"), hbm("uy", s_[:, :]))])
    ms(whole("pqi"), 0)
    dma("sync", [(r("pqi", s_[0:128:16, :]), hbm("px", s_[:, :])), (r("pqi", s_[1:128:16, :]), hbm("py", s_[:, :]))])
    for h, q in ((0, "sync"), (1, "a")):
        dma(q, [(r("lri", s_[(i % 2) * 64:(i % 2) * 64 + 64, (i // 2) * 48:(i // 2) * 48 + 48]), hbm("nb", s_[i:128:16, :]))
                for i in range(8 * h, 8 * h + 8)])
    dma("sync", [(whole("nbi"), hbm("nb", s_[:, :]))])
    dma("sync", [(r("WT", s_[:, 0:V]), hbm("wt", s_[:, :]))])

    bd = r("bdu", s_[:, 0:6])
    cp(bd, r("bdi", s_[:, 0:6]))
    for c in range(2):
        ts(r("msg", s_[:, 0, c * B:c * B + B]), ind(whole("xi%d" % c), bd), 0.0, None, A.add)
    ts(r("msg", s_[:, 0, 2 * B:3 * B]), ind(whole("pqi"), bd), 0.0, None, A.add)
    exchange(0, r("msg", s_[:, 0, :]), [r("land0", s_[:, :, :])], cfg.get("xlat0", 9000))
    act(whole("wmsg"), ind(r("WT", s_[:, 0:V]), bd), F.Identity)
    exchange(3, whole("wmsg"), [r("WT", s_[:, V:E])], 9000)

    iota(r("pc", s_[:, 0:1]), [[0, 1]], 0, 1)
    iota(whole("io"), [[1, 128]], 0, 0)
    iota(r("cg", s_[:, 0, :]), [[16, 8], [0, 16]], 0, 0)
    iota(r("cg", s_[:, 1, :]), [[8, 16], [0, 8]], 0, 0)
    for j, m in ((1, 112), (2, 15), (3, 7), (6, 8), (7, 120)):
        ts(r("pc", s_[:, j:j + 1]), r("pc", s_[:, 0:1]), m, None, A.bitwise_and)
    ms(r("pc", s_[:, 4:6]), 0)
    cp(r("pf", s_[:, 0:8]), whole("pc"))
    ts(col(4), col(6), 0.0, None, A.is_equal)
    ts(col(5), col(6), 8.0, None, A.is_equal)
    ts(col(9), col(3), col(4), 2304.0, A.mult, A.mult)
    io = whole("io")
    ts(I, io, col(0), None, A.is_equal)
    ts(nI, io, col(0), -1.0, A.is_equal, A.mult)
    ts(I32, io, col(0), None, A.is_equal)
    ts(BO, r("cg", s_[:, 0, :]), col(1), None, A.is_equal)
    ts(whole("B8"), r("cg", s_[:, 1, :]), col(7), None, A.is_equal)
    ts(whole("BOs"), BO, 32768.0, None, A.mult)
    ts(whole("BO2"), BO, 2048.0, None, A.mult)
    ts(whole("LOs"), BO, col(4), 1048576.0, A.mult, A.mult)
    ts(whole("nLO2"), BO, col(4), -2048.0, A.mult, A.mult)
    ts(r("mk", s_[:, 0:16]), r("io", s_[:, 0:16]), col(2), None, A.is_equal)
    ts(r("mk", s_[:, 16:24]), r("io", s_[:, 0:8]), col(3), None, A.is_equal)
    if cfg["pool"]:
        ms(whole("neg"), -1.0)
        ms(whole("one"), 1.0)
    for k in range(8):
        if cfg["pool"] & 1:
            asel(r("nSel", s_[:, k, :]), whole("neg"), [[-16, 8], [0, 16]], A.is_equal, -k, 1)
        else:
            ts(r("nSel", s_[:, k, :]), BO, r("mk", s_[:, k:k + 1]), -1.0, A.mult, A.mult)
        if cfg["pool"] & 2:
            asel(r("BJ", s_[:, k, :]), whole("one"), [[-8, 16], [0, 8]], A.is_equal, -k, 1)
        else:
            ts(r("BJ", s_[:, k, :]), whole("B8"), r("mk", s_[:, 16 + k:17 + k]), None, A.mult)
    for k in range(2):
        ts(r("Sel", s_[:, k, :]), BO, r("mk", s_[:, k:k + 1]), None, A.mult)
        ts(r("nD", s_[:, k, :]), nI, col(4 + k), None, A.mult)
    tt(SPQ, r("Sel", s_[:, 0, :]), r("Sel", s_[:, 1, :]), A.add)
    ms(whole("R"), 0.0)
    ts(r("R", s_[:, 7:135:8]), r("BO", s_[:, 0:128:8]), 512.0, None, A.mult)
    ts(BO1, BO, 1024.0, None, A.mult)
    ms(r("BG", s_[:, :, :]), 0.0)
    ts(r("BG", s_[:, :, 15:143:16]), r("nSel", s_[:, :, 0:128:16]), -1.0, None, A.mult)
    ms(whole("KB"), 0.0)
    ts(r("KB", s_[:, 15:143:16]), r("BO", s_[:, 0:128:16]), col(9), None, A.mult)
    if not cfg["pool"]:
        ms(whole("one"), 1.0)
    for h in range(2):
        asel(r("EX", s_[:, h, :]), whole("one"), [[-8, 8], [0, 2], [-1, 8]], A.is_equal, -64 * h, 1)
    asel(whole("IT"), BO, [[16, 8], [0, 2], [1, 8]], A.is_ge, -1, -1)
    tt(whole("IT"), I, whole("IT"), A.subtract)
    iota(r("NX", s_[:, 1, 0:V]), [[-2048, 8], [0, B]], 7 * 2048 + E, 0)
    act(whole("KC"), r("NX", s_[:, 1, 0:V]), F.Identity)
    io96 = r("io", s_[:, 0:B])
    ts(whole("DUM"), io96, float(2 ** 20 + 8 * 32768 + 16384 + V), None, A.add)
    ts(whole("dm"), io96, float(V - 2048), None, A.add)
    iota(r("sm", s_[:, 0, :]), [[0, 6], [1, 16]], 0, 0)
    ts(r("TM", s_[:, :, :]), r("sm", s_[:, 0, :]), col(2), None, A.is_gt)
    iota(whole("spf"), [[0, 8], [-16, 48]], E, 0)
    ts(whole("sp"), whole("spf"), col(2), None, A.subtract)
    ts(r("sm", s_[:, 1, 0:48]), r("io", s_[:, 0:48]), 16.0, None, A.mult)
    for j, w in enumerate((TBW, 6144)):
        ts(r("TR", s_[:, j, 0:12]), r("sm", s_[:, 1, 0:12]), col(2), float(w), A.add, A.add)
    ts(r("sm", s_[:, 2, 0:6]), r("sm", s_[:, 1, 0:6]), col(2), 8.0, A.add, A.mult)
    for t in range(3):
        ts(r("vw", s_[:, t, :]), r("sm", s_[:, 1, 0:48]), col(6), float(7 - t), A.add, A.add)
        if t < 2:
            ts(r("EV", s_[:, t, :]), io96, -8.0, float(E - 7 + t), A.mult, A.add)
            ts(r("vp", s_[:, t, 0:6]), r("sm", s_[:, 2, 0:6]), float(7 - t), None, A.add)
    ms(r("Lp", s_[:, V:784]), 0.0)
    ms(r("Fb", s_[:, V:864]), 0.0)
    ms(r("TB", s_[:, TBW:TBW + 960]), 0.0)
    ms(r("NX", s_[:, :, V:864]), 0.0)
    ms(whole("c9"), 0.28125)
    ts(whole("I5"), I, 32.0, None, A.mult)

    for c in range(2):
        if cfg["act_int"]:
            act(r("XY", s_[:, c, 0:V]), whole("xi%d" % c), F.Identity, bias=MG)
        else:
            ts(r("XY", s_[:, c, 0:V]), whole("xi%d" % c), MG, None, A.add)
        act(r("H", s_[:, c, :]), r("XY", s_[:, c, 0:V]), F.Identity, bias=-MG)
    dma("sync", [(whole("ldi"), hbm("ld", s_[:, :]))])
    for o, i in ((r("PQ", s_[:, 0:V]), whole("pqi")), (whole("PQh"), whole("pqi")), (whole("ldh"), whole("ldi"))):
        if cfg["act_int"]:
            act(o, i, F.Identity)
        else:
            cp(o, i)

    def zero(o):
        if cfg["zero_g"]:
            iota(o, [[0, count(o, units)]], 0, 0)
        else:
            act(o, whole("KC"), F.Identity, scale=0.0)
    act(r("ACC", s_[:, :, 768:1152]), whole("KC"), F.Identity, scale=0.0)
    ts(whole("lrh"), whole("lri"), -1.0, float(E), A.mult, A.add)
    u = unit(2)
    pe([(ps(u, s_[i:384:16], b), r("EX", s_[:, i % 2, :]), r("lrh", s_[:, (i // 2) * 48 + 24 * b:(i // 2) * 48 + 24 * b + 24]), True, True)
        for b in range(2) for i in range(16)])
    act(whole("Lh"), ps(u, s_[0:384]), F.Identity)
    cp(r("Lp", s_[:, 0:V]), ps(u, s_[0:384]))
    wa = [whole("w%d" % j) for j in range(3)]
    if cfg["pre0"]:
        ts(wa[0], whole("nbi"), float(E), 2048.0, A.is_equal, A.mult)
        tt(wa[1], wa[0], whole("sp"), A.min)
        tt(wa[2], whole("nbi"), wa[1], A.subtract)
        cp(r("Wu", s_[:, 3, :]), wa[2])

    def unpack(t):
        for c in range(2):
            if c < cfg["unp_v"]:
                ts(r("XY", s_[:, c, V:E]), r("land%d" % t, s_[:, :, c * B:c * B + B]), MG, None, A.add)
            else:
                act(r("XY", s_[:, c, V:E]), r("land%d" % t, s_[:, :, c * B:c * B + B]), F.Identity, bias=MG)
        if t == 0:
            cp(r("PQ", s_[:, V:E]), r("land0", s_[:, :, 2 * B:3 * B]))

    order = [(hv, k) for hv in range(2) for k in range(8)]

    def lst(w, hv, k):
        return r("Wu", s_[:, w, k * 48 + hv * 24:k * 48 + hv * 24 + 24])

    def tables(w):
        for n, (hv, k) in enumerate(order):
            v0, tb, q0 = 384 * hv, (2 * k + hv) * 1152, (2 * k + hv) * 384
            dd, sq = r("Q", s_[:, q0:q0 + 384]), r("MM", s_[:, 0, q0:q0 + 384])
            own = r("PQh", s_[:, v0:v0 + 384])
            if cfg["tpe"]:
                sq = r("TB", s_[:, tb + 768:tb + 1152])
            if n % 4 < cfg["init_g"]:
                act(dd, ind(whole("PQ"), lst(w, hv, k)), F.Identity)
                u0 = ps(unit(), s_[0:384])
                pe(grp(u0, [(nI, own), (I, dd)]))
                act(sq, u0, F.Square, scale=8.0)
                u1, u2 = unit(2), unit()
                pe([m for c in range(2) for m in grp(ps(u1, s_[0:384], c), [(r("nSel", s_[:, c, :]), own), (r("Sel", s_[:, c, :]), dd)])])
            else:
                tt(dd, ind(whole("PQ"), lst(w, hv, k)), own, A.subtract)
                act(sq, dd, F.Square, scale=8.0)
                u1, u2 = unit(2), unit()
                pe([(ps(u1, s_[0:384], c), r("Sel", s_[:, c, :]), dd, True, True) for c in range(2)])
            if not cfg["tpe"]:
                pe([(ps(u2, s_[0:384]), SPQ, sq, True, True)])
            if n % 4 < cfg["init_v2"]:
                cp(r("TB", s_[:, tb:tb + 768]), ps(u1, s_[0:384]))
            else:
                act(r("TB", s_[:, tb:tb + 768]), ps(u1, s_[0:384]), F.Identity)
            if cfg["tpe"]:
                continue
            if n % 4 < cfg["init_v"]:
                cp(r("TB", s_[:, tb + 768:tb + 1152]), ps(u2, s_[0:384]))
            else:
                act(r("TB", s_[:, tb + 768:tb + 1152]), ps(u2, s_[0:384]), F.Identity)

    def relist(t, rows):
        for pc in range(4):
            u = unit()
            for k in (2 * pc, 2 * pc + 1):
                pe(grp(ps(u, s_[(k % 2) * 48:(k % 2) * 48 + 48]), [(bg(k, i), r(rows, s_[:, i:V:16])) for i in range(16)]))
            c = s_[:, pc * B:pc * B + B]
            w = [r("wa", s_[:, j, pc % 2 * B:pc % 2 * B + B]) for j in range(3)]
            act(w[0], ps(u, s_[0:B]), F.Relu, scale=-2048.0, bias=2048.0)
            tt(w[1], w[0], r("sp", c), A.min)
            tt(w[2], ps(u, s_[0:B]), w[1], A.add)
            ts(r("Wu", s_[:, t, pc * B:pc * B + B]), w[2], -1.0, float(E), A.mult, A.add)

    def step1(t):
        rho = 7 - t
        xy, hh = "XY", "H"

        def kc(u, k):
            return ps(u, s_[(k % 4) * B:(k % 4) * B + B], k // 4)
        act(whole("em"), whole("Lh"), F.Relu, scale=-1.0, bias=1.0)
        u = unit(2)
        pe([(ps(u, s_[0:384], b), whole("IT"), r("em", s_[:, 384 * b:384 * b + 384]), True, True) for b in range(2)])
        act(r("Fb", s_[:, 0:V]), ps(u, s_[0:384]), F.Relu)
        Fa = r("Fb", s_[:, rho:V:8])
        u = unit()
        pe(grp(ps(u, s_[0:48]), [(r("nD", s_[:, h, :]), r("Lh", s_[:, rho + 8 * h:V:16])) for h in range(2)]))
        ts(whole("o1"), ps(u, s_[0:48]), float(E), float(V), A.add, A.min)
        ts(whole("Uc"), ps(u, s_[0:48]), float(E), float(V), A.add, A.min)
        act(whole("G"), ind(r("Lp", s_[:, 0:V + 1]), whole("o1")), F.Identity)
        u = unit()
        pe(grp(ps(u, s_[0:48]), [(bg((i % 8 + t) % 8, i), r("G", s_[:, i:V:16])) for i in range(16)]))
        c16 = whole("c16")
        act(c16, ps(u, s_[0:48]), F.Identity, scale=-1.0, bias=float(E))
        ts(r("ci", s_[:, 0, :]), ps(u, s_[0:48]), -1.0, float(E), A.mult, A.add)
        ts(r("ci", s_[:, 1, :]), r("ci", s_[:, 0, :]), 7, None, A.bitwise_and)
        ts(r("e12", s_[:, 0, :]), r("ci", s_[:, 1, :]), float(rho), None, A.is_equal)
        ts(r("e12", s_[:, 1, :]), c16, float(V), None, A.is_ge)
        tt(r("dv", s_[:, 0, :]), r("vw", s_[:, t, :]), c16, A.subtract)
        u = unit()
        pe([m for j in range(8) for m in grp(ps(u, s_[j * 48:j * 48 + 48]), [(r("BJ", s_[:, j, :]), whole("Uc")), (nI, c16)])])
        ts(whole("eq"), ps(u, s_[0:384]), 0.0, None, A.is_equal)
        u = unit()
        pe(grp(ps(u, s_[0:48]), [(I, r("e12", s_[:, j, :])) for j in range(2)] + [(I, r("eq", s_[:, j * 48:j * 48 + 48])) for j in range(8)]))
        d1 = r("dv", s_[:, 1, :])
        ts(d1, ps(u, s_[0:48]), 1.0, None, A.min)
        tt(d1, d1, r("dv", s_[:, 0, :]), A.mult)
        tt(d1, d1, c16, A.add)
        cp(whole("o2"), d1)
        act(whole("GP"), ind(r("PQ", s_[:, 0:V]), whole("o2")), F.Identity)
        pa = r("PQh", s_[:, rho:V:8])
        for c, (w, nw) in enumerate(((r("Sel", s_[:, 0, :]), r("nSel", s_[:, 0, :])), (r("Sel", s_[:, 1, :]), r("nSel", s_[:, 1, :])), (I, nI))):
            u = unit(2)
            pe([m for k in range(8) for m in grp(kc(u, k), [(w, r("GP", s_[:, k:V:8])), (nw, pa)])])
            if c < cfg["ct_v"]:
                cp(r("CT", s_[:, c, :]), ps(u, s_[0:384]))
            elif c < 2:
                act(r("CT", s_[:, c, :]), ps(u, s_[0:384]), F.Identity)
            else:
                act(whole("csq"), ps(u, s_[0:384]), F.Square, scale=8.0)
        u = unit(2)
        pe([(ps(u, s_[0:384], b), SPQ, r("csq", s_[:, 384 * b:384 * b + 384]), True, True) for b in range(2)])
        act(r("CT", s_[:, 2, :]), ps(u, s_[0:384]), F.Identity)
        act(r("gc2", s_[:, 0, :]), ind(r(xy, s_[:, 0, 0:V]), whole("o2")), F.Identity, bias=-MG)
        if cfg["gy_v"]:
            ts(r("gc2", s_[:, 1, :]), ind(r(xy, s_[:, 1, 0:V]), whole("o2")), -MG, None, A.add)
        else:
            act(r("gc2", s_[:, 1, :]), ind(r(xy, s_[:, 1, 0:V]), whole("o2")), F.Identity, bias=-MG)
        keys = []
        for b in range(2):
            hb = s_[384 * b:384 * b + 384]
            uu = [unit(), unit()]
            for c in (1, 0):
                pe([m for k in range(4 * b, 4 * b + 4) for m in grp(ps(uu[c], s_[(k % 4) * B:(k % 4) * B + B]),
                    [(I, r("gc2", s_[:, c, k:V:8])), (nI, r(hh, s_[:, c, rho:V:8]))])])
            z = ps(uu[0], s_[0:384])
            tt(r("cb", s_[:, hb]), ps(uu[1], s_[0:384]), r("CT", s_[:, 1, hb]), A.mult)
            tt(z, z, r("CT", s_[:, 0, hb]), A.mult)
            tt(z, z, r("cb", s_[:, hb]), A.add)
            act(z, z, F.Abs)
            tt(r("ind", s_[:, hb]), z, r("CT", s_[:, 2, hb]), A.is_gt)
            u = unit(1, 0)
            keys.append(ps(u, s_[0:384]))
            mm = [(keys[b], I, r("KC", s_[:, hb]), True, False)]
            for k in range(4 * b, 4 * b + 4):
                o = ps(u, s_[(k % 4) * B:(k % 4) * B + B])
                mm += [(o, r("nSel", s_[:, (k + t) % 8, :]), r("G", s_[:, k:V:8]), False, False), (o, whole("LOs"), Fa, False, False)]
            mm.append((keys[b], whole("BOs"), r("ind", s_[:, hb]), False, True))
            pe(mm)
            if b == 0:
                if not cfg["tree"]:
                    act(whole("ev"), keys[0], F.Identity)
                if cfg["tree"]:
                    for j in range(4):
                        tt(r("m1", s_[:, j * B:j * B + B]), ps(u, s_[j * B:j * B + B]), r("m1", s_[:, j * B - B:j * B]) if j else whole("DUM"), A.max)
        if cfg["tree"]:
            for j in range(4):
                tt(r("bi", s_[:, 0, :]) if j == 3 else r("m2", s_[:, j * B:j * B + B]), ps(u, s_[j * B:j * B + B]),
                   r("m2", s_[:, j * B - B:j * B]) if j else r("m1", s_[:, 288:384]), A.max)
        else:
            tt(whole("m1"), keys[1], whole("ev"), A.max)
            tt(r("m2", s_[:, 0:192]), r("m1", s_[:, 0:192]), r("m1", s_[:, 192:384]), A.max)
            tt(r("m2", s_[:, 192:288]), r("m2", s_[:, 0:B]), r("m2", s_[:, B:192]), A.max)
            tt(r("bi", s_[:, 0, :]), r("m2", s_[:, 192:288]), whole("DUM"), A.max)
        ts(r("bi", s_[:, 1, :]), r("bi", s_[:, 0, :]), 2047, None, A.bitwise_and)
        n16 = whole("n16")
        cp(n16, r("bi", s_[:, 1, :]))
        u = unit()
        diag(ps(u, s_[0:6]), lambda i: r("n16", s_[:, i:B:16]))
        cp(r("cwf", s_[:, 0:6]), ps(u, s_[0:6]))
        cp(r("o3", s_[:, 0:6]), ps(u, s_[0:6]))
        act(whole("Fc"), ind(whole("Fb"), r("o3", s_[:, 0:6])), F.Identity)
        for b in range(6):
            ts(r("EQ", s_[:, b, 0:B - 16 * b]), r("n16", s_[:, 16 * b:B]), r("cwf", s_[:, b:b + 1]), None, A.is_equal)
        tt(r("EQ", s_[:, :, 0:16]), r("EQ", s_[:, :, 0:16]), r("TM", s_[:, :, :]), A.mult)
        u = unit()
        pe([(ps(u, s_[0:B]), I, n16, True, False), (ps(u, s_[0:B]), whole("nLO2"), whole("Fc"), False, False)]
           + [(ps(u, s_[16 * b:B]), whole("BO2"), r("EQ", s_[:, b, 0:B - 16 * b]), False, False) for b in range(5, 0, -1)]
           + [(ps(u, s_[0:B]), whole("BO2"), r("EQ", s_[:, 0, 0:B]), False, True)])
        n2 = whole("n2")
        tt(n2, ps(u, s_[0:B]), whole("dm"), A.min)
        u = unit()
        diag(ps(u, s_[0:6]), lambda i: r("n2", s_[:, i:B:16]))
        o4 = r("o4", s_[:, 0:6])
        ts(o4, ps(u, s_[0:6]), 2048.0, None, A.add)
        tq = [r("t96", s_[:, j, :]) for j in (0, 1, 2, 3, 4, 5, 6, 7, 0, 1, 2)]
        bq = [r("b96", s_[:, j, :]) for j in range(4)]
        sel = [r("Sel", s_[:, c, :]) for c in range(2)]
        nsel = [r("nSel", s_[:, c, :]) for c in range(2)]
        if t < 2:
            enter(t, u, n2, o4, tq, bq, sel, nsel)
            return
        for c in range(3):
            zero(r("NX", s_[:, c, 0:V]))
        tt(bq[0], ind(r("PQ", s_[:, 0:864]), o4), r("PQh", s_[:, rho:V:8]), A.subtract)
        act(bq[1], bq[0], F.Square, scale=8.0)
        u = unit()
        pq = [ps(u, s_[j * B:j * B + B]) for j in range(4)]
        pe([(pq[0], sel[0], bq[0], True, True), (pq[1], sel[1], bq[0], True, True), (pq[2], SPQ, bq[1], True, True)]
           + grp(pq[3], [(nsel[0], bq[1]), (nsel[1], bq[1])]))
        for c in range(2):
            act(tq[6 + c], r(xy, s_[:, c, rho:V:8]), F.Identity)
            tt(tq[c], ind(r(xy, s_[:, c, 0:864]), o4), tq[6 + c], A.subtract)
            tt(tq[c], tq[c], pq[c], A.mult)
        tt(tq[0], tq[0], tq[1], A.add)
        tt(tq[2], tq[0], pq[2], A.min)
        tt(tq[2], tq[2], pq[3], A.max)
        tt(tq[0], tq[0], tq[2], A.subtract)
        ts(tq[0], tq[0], -1023.0, 1023.0, A.max, A.min)
        ts(bq[2], tq[0], 0.0, None, A.not_equal)
        ts(bq[3], n2, float(V - 2048), 16.0, A.is_ge, A.mult)
        u = unit(1, 0)
        pe(grp(ps(u, s_[0:B]), [(nI, bq[3]), (BO, bq[2])]))
        ts(tq[3], ps(u, s_[0:B]), 3.5, None, A.is_ge)
        tt(tq[4], tq[0], tq[3], A.mult)
        act(tq[5], tq[4], F.Abs)
        for c in range(2):
            tt(tq[6 + c], tq[4], pq[c], A.mult)
            act(r("NX", s_[:, c, rho:V:8]), tq[6 + c], F.Identity)
            ts(ind(r("NX", s_[:, c, :]), o4), tq[6 + c], -1.0, 0.0, A.mult, A.add)
        tt(tq[8], ind(r("WT", s_[:, 0:864]), o4), tq[5], A.mult)
        act(r("NX", s_[:, 2, rho:V:8]), tq[8], F.Identity)
        tt(ind(r("NX", s_[:, 2, :]), o4), tq[5], r("WT", s_[:, rho:V:8]), A.mult)

    def enter(t, u, n2, o4, tq, bq, sel, nsel):
        rho = 7 - t
        nw = r("tw", s_[:, 0, 6:12])
        nd = r("NX", s_[:, 0, :])
        patch = t > 0 or cfg["pre0"]
        if patch:
            act(nw, ps(u, s_[0:6]), F.Identity, bias=2048.0)
        zero(r("NX", s_[:, 0, 0:V]))
        act(tq[0], n2, F.Identity, scale=-1.0, bias=float(E - 2048))
        ts(tq[1], n2, float(V - 2048), None, A.is_lt)
        cp(ind(nd, o4), r("EV", s_[:, t, :]))
        tt(r("NX", s_[:, 0, rho:V:8]), tq[0], tq[1], A.mult)
        u = unit(2)
        pe([(ps(u, s_[0:384], b), I, r("Fb", s_[:, 384 * b:384 * b + 384]), True, True) for b in range(2)])
        tt(ps(u, s_[0:384]), ps(u, s_[0:384]), r("NX", s_[:, 0, 0:V]), A.mult)
        tt(whole("Lh"), ps(u, s_[0:384]), whole("Lh"), A.add)
        relist(t, "Lh")
        if not patch:
            return
        tt(bq[0], ind(r("PQ", s_[:, 0:864]), o4), r("PQh", s_[:, rho:V:8]), A.subtract)
        act(bq[1], bq[0], F.Square, scale=8.0)
        u = unit()
        pe([(ps(u, s_[j * B:j * B + B]), w, bq[0], True, True) for j, w in enumerate((sel[0], nsel[0], sel[1], nsel[1]))]
           + [(ps(u, s_[384:480]), I if cfg["tpe"] else SPQ, bq[1], True, True)])
        act(r("VAL", s_[:, 0:480]), ps(u, s_[0:480]), F.Identity)
        act(r("VAL", s_[:, 480:576]), ps(u, s_[384:480]), F.Identity)
        u = unit()
        pe(grp(ps(u, s_[0:6]), [(r("KB", s_[:, 15 - i:143 - i]), r("Fb", s_[:, rho + 8 * i:V:128])) for i in range(16)])
           + grp(ps(u, s_[6:12]), [(r("KB", s_[:, 15 - i:143 - i]), r("Fc", s_[:, i:B:16])) for i in range(16)]))
        w = [r("tw", s_[:, j, 0:12]) for j in range(6)]
        act(r("tw", s_[:, 0, 0:6]), r("vp", s_[:, t, 0:6]), F.Identity)
        for c in range(2):
            ts(r("tw", s_[:, 1, 6 * c:6 * c + 6]), nw, float(V), 32768.0, A.is_ge, A.mult)
        ts(w[2], w[0], 384.0, 768.0, A.is_ge, A.mult)
        tt(w[1], w[1], w[0], A.add)
        tt(w[3], ps(u, s_[0:12]), w[2], A.add)
        tt(w[4], w[3], w[1], A.add)
        tt(w[4], w[4], r("TR", s_[:, 0, 0:12]), A.min)
        for c in range(3):
            ts(r("o5", s_[:, 12 * c:12 * c + 12]), w[4], 384.0 * c, None, A.add)
        cp(ind(whole("TB"), r("o5", s_[:, 0:36])), whole("VAL"))

    def forces(t):
        xy, hh, ups = "XY", "H", []
        row, late = None, []
        for n, (hv, k) in enumerate(order):
            d, dp, v0, cb = n % ND_, n % NP_, 384 * hv, 2 * k + hv
            vs = s_[v0:v0 + 384]
            tb, sl = cb * 1152, s_[cb * 384:cb * 384 + 384]
            if k == 0:
                act(r("ACC", s_[:, hv, 0:384]), r(hh, s_[:, 0, vs]), F.Identity, scale=32.0, bias=0.5)
                o = ps(unit(), s_[0:384])
                pe(grp(o, [(whole("I5"), r(hh, s_[:, 1, vs])), (I, r("ldh", s_[:, vs]))]))
                act(r("ACC", s_[:, hv, 384:768]), o, F.Identity, bias=0.5)
            u = unit(2)
            dg, da = n % NG_, n % NA_
            for c in range(2):
                act(r("gx", s_[:, dg, c, :]), ind(r(xy, s_[:, c, :]), lst(t, hv, k)), F.Identity, bias=-MG)
                o = ps(unit(), s_[0:384]) if cfg["ab_split"] else ps(u, s_[0:384], c)
                pe(grp(o, [(nI, r(hh, s_[:, c, vs])), (I, r("gx", s_[:, dg, c, :]))]))
                if cfg["ab_split"]:
                    tt(r("ab", s_[:, da, 384 * c:384 * c + 384]), o, r("TB", s_[:, tb + 384 * c:tb + 384 * c + 384]), A.mult)
            if not cfg["ab_split"]:
                tt(r("ab", s_[:, da, :]), ps(u, s_[0:384]), r("TB", s_[:, tb:tb + 768]), A.mult)
            z, sp_, cn = ps(unit(), s_[0:384]), ps(unit(1, 0), s_[0:384]), ps(unit(1, 0), s_[0:384])
            sg = r("Q", s_[:, sl]) if cfg["sg"] else sp_
            ea, eb = r("ab", s_[:, da, 0:384]), r("ab", s_[:, da, 384:768])
            if n % 4 < cfg["ab_dma"][t]:
                dma("gq", [(ea, eb)], True)
                pe(grp(z, ([(I, r("Q", s_[:, sl]))] if t else []) + [(I32, ea)]))
            else:
                pe(grp(z, ([(I, r("Q", s_[:, sl]))] if t else []) + [(I32, ea), (I32, eb)]))
            sgn = act(sg, z, F.Sign)
            amt, nz = r("amt", s_[:, d, :]), r("nz", s_[:, d, :])
            mc, pen = amt, (n + 2) % 4 < cfg["pen"][t]
            if cfg["tpe"]:
                act(eb, z, F.Abs)
                o = ps(unit(1, 0), s_[0:384])
                nodes[pe([(o, SPQ, r("TB", s_[:, tb + 768:tb + 1152]), True, True)])]["deps"].add(sgn)
                tt(amt, eb, o, A.subtract)
            else:
                act(z, z, F.Abs)
                tt(amt, z, r("TB", s_[:, tb + 768:tb + 1152]), A.subtract)
            if (n % 4) < cfg["nz_act"][t]:
                act(nz, amt, F.Sign, bias=-0.5)
                pe(grp(cn, [(BO2, whole("c9"))] * (not pen) + [(BO1, nz)]))
                off = 9216.0
            else:
                ts(nz, amt, 0.0, 0.21875, A.is_gt, A.subtract)
                pe([(cn, BO2, nz, True, True)])
                off = 0.0
            mm = r("MM", s_[:, t, sl]) if t < 2 else amt
            if pen:
                act(nz, cn, F.Relu, scale=-32.0, bias=-32.0 * off)
                o = ps(unit(1, 0), s_[0:384])
                pe(grp(o, [(I, amt), (nI, nz)]))
                ts(mm, o, 0.0, 1023.0, A.max, A.min)
            else:
                tt(mc, cn, amt, A.min)
            if pen:
                pass
            elif n % 4 < cfg["clip_act"][t]:
                act(mc, mc, F.Relu, scale=-1.0, bias=1023.0)
                act(mm, mc, F.Relu, scale=-1.0, bias=1023.0)
            else:
                ts(mm, mc, 0.0, 1023.0, A.max, A.min)
            if cfg["sg"] == 1:
                pe([(sp_, I, sg, True, True)])
                sg = sp_
            if t < 2:
                tt(r("Q", s_[:, sl]), sg, mm, A.mult)
                if cfg["p2"]:
                    u = unit(2, 0)
                    pe([(ps(u, s_[0:384], c), I, r("Q", s_[:, sl]), True, True) for c in range(2)])
                    tt(r("P", s_[:, dp, 0:768]), ps(u, s_[0:384]), r("TB", s_[:, tb:tb + 768]), A.mult)
                else:
                    qp = ps(unit(1, 0), s_[0:384])
                    pe([(qp, I, r("Q", s_[:, sl]), True, True)])
            else:
                qp = sp_
                tt(qp, sg, mm, A.mult)
            for c in range(0 if t < 2 and cfg["p2"] else 2):
                tt(r("P", s_[:, dp, 384 * c:384 * c + 384]), qp, r("TB", s_[:, tb + 384 * c:tb + 384 * c + 384]), A.mult)
            w = 768
            if t == 2:
                um = ps(unit(1, 0), s_[0:384])
                pw = r("P", s_[:, dp, 768:1152])
                act(pw, ind(whole("WT"), lst(1, hv, k)), F.Identity)
                pe(grp(um, [(I, r("MM", s_[:, 0, sl])), (I, r("MM", s_[:, 1, sl])), (I, mm)]))
                tt(pw, um, pw, A.mult)
                w = 1152
            how = cfg["sum"][hv][k]
            if how == "p":
                late.append(dp)
            elif how == "b":
                dq = (n - 1) % NP_
                dma("gq", [(r("P", s_[:, dq, 0:w]), r("P", s_[:, dp, 0:w]))], True)
                dma("gq", [(r("ACC", s_[:, hv, 0:w]), r("P", s_[:, dq, 0:w]))], True)
            elif how == "c":
                dma("gq", [(r("ACC", s_[:, hv, 0:w]), r("P", s_[:, dp, 0:w]))], True)
            if t == 2 and k == (7 if hv == 0 else cfg["nx1"]):
                dma("gq", [(r("ACC", s_[:, hv, :]), r("NX", s_[:, :, vs]))], True)
            if k < 7:
                continue
            if t < 2:
                row = ps(unit(), s_[0:384])
                terms = [(r("R", s_[:, 7 - j:135 - j]), r("MM", s_[:, t, (2 * j + hv) * 384:(2 * j + hv) * 384 + 384])) for j in range(8)]
                pe(grp(row, terms[:7], True, False))
                pe(grp(row, terms[7:], False, True))
                tt(r("Lp", s_[:, vs]), row, r("Lh", s_[:, vs]), A.min)
                act(r("Lh", s_[:, vs]), r("Lp", s_[:, vs]), F.Identity)
            src = [r("ACC", s_[:, hv, 384 * c:384 * c + 384]) for c in range(3)]
            if late:
                for c in range(3 if t == 2 else 2):
                    o = ps(unit(), s_[0:384])
                    terms = [(I32, r("P", s_[:, x, 384 * c:384 * c + 384])) for x in late]
                    terms.insert(len(late) - 1, (I32, src[c]))
                    if cfg["nx1"] < 0 and t == 2:
                        terms.insert(0, (I32, r("NX", s_[:, c, vs])))
                    nv = cfg["vlast"]
                    for j, x in enumerate(terms[:len(terms) - nv]):
                        pe(grp(o, [x], j == 0, j == len(terms) - nv - 1))
                    for x in terms[len(terms) - nv:]:
                        tt(o, o, x[1], A.add)
                    src[c] = o
                late = []
            for c in range(2):
                up = src[c]
                act(up, src[c], F.Identity, scale=0.03125, bias=MG)
                if t < 2:
                    ups.append((c, vs, up))
                else:
                    ts(up, up, MG - 1023.0, MG + 1023.0, A.max, A.min)
                    o = r("ACC", s_[:, hv, 384 * c:384 * c + 384])
                    act(o, up, F.Identity, bias=-MG)
                    dma("sync", [(hbm(("yx", "yy")[c], s_[:, vs]), o)])
            if t == 2:
                o = r("ACC", s_[:, hv, 768:1152])
                if src[2][0] == "p":
                    act(o, src[2], F.Identity)
                dma("sync", [(hbm("yw", s_[:, vs]), o)])
        if t < 2:
            for c, vs, up in ups:
                ts(r(xy, s_[:, c, vs]), up, MG - 1023.0, MG + 1023.0, A.max, A.min)
                act(r(hh, s_[:, c, vs]), r(xy, s_[:, c, vs]), F.Identity, bias=-MG)
            for c in range(2):
                o, i = r("msg", s_[:, 1 - t, c * B:c * B + B]), ind(r(xy, s_[:, c, 0:V]), bd)
                if c:
                    ts(o, i, -MG, None, A.add)
                else:
                    act(o, i, F.Identity, bias=-MG)
            exchange(t + 1, r("msg", s_[:, 1 - t, 0:192]), [r("land%d" % (t + 1), s_[:, :, :])], cfg.get("xlat", 7000))

    unpack(0)
    if cfg["pre0"]:
        tables(3)
    for t in range(3):
        first = len(nodes)
        step1(t)
        for x in nodes[first:]:
            x["early"] = cfg["early"][t]
        if t == 0 and not cfg["pre0"]:
            tables(0)
        forces(t)
        if t == 1:
            relist(2, "Lh")
        if t < 2:
            unpack(t + 1)
    return nodes, units


def place(nodes, units, cfg, prio, back=False):
    n = len(nodes)
    hop, grain = cfg["hop"], cfg["grain"]
    pred = [x["pre"] for x in nodes]
    succ = [x["suc"] for x in nodes]
    if back:
        pred, succ = succ, pred
    left = [len(x) for x in pred]
    ready = [j for j in range(n) if left[j] == 0]
    fin, rdy, start = [0.0] * n, [0.0] * n, [0.0] * n
    free = {}
    banks = [(0.0, []) for _ in range(cfg["banks"])]
    idle = list(range(cfg["banks"]))
    todo = [len(u["nodes"]) for u in units]
    phys = [None] * len(units)
    out, extra = [], {}
    while ready:
        best, can = None, []
        if not back:
            wait = [(prio[j], u) for j in ready for u in nodes[j]["units"] if phys[u] is None]
            first = min(wait)[1] if wait else None
            since = sorted(banks[b][0] for b in idle)
            pairs = sorted((max(banks[b][0], banks[b + 1][0]), b) for b in idle if b + 1 in idle)
        for j in ready:
            x = nodes[j]
            st = rdy[j] + (x["lat"] if back else 0.0)
            if x["eng"]:
                st = max(st, free.get(x["eng"], 0.0))
            new = () if back else [u for u in x["units"] if phys[u] is None]
            if new:
                need = sum(units[u]["n"] for u in new)
                keep = max(units[u]["resv"] for u in new)
                if keep and first not in new:
                    keep = max(keep, units[first]["n"] + cfg["resv2"])
                if len(idle) < need + keep or (need == 2 and not pairs):
                    continue
                st = max(st, (pairs[0][0] if need == 2 else since[0]) + hop)
            key = (int(st / grain), prio[j])
            can.append((key, j, st, new))
            if best is None or key < best[0]:
                best = can[-1]
        if best is None:
            return None
        if not back and cfg["slack"]:
            x = nodes[best[1]]
            for c in can:
                if nodes[c[1]]["eng"] == x["eng"] and prio[c[1]] + cfg["slack"] < prio[best[1]] and c[2] < best[2] + x["cost"] * cfg["part"]:
                    best, x = c, nodes[c[1]]
        _, j, st, new = best
        x = nodes[j]
        for u in sorted(new):
            if units[u]["n"] == 2:
                phys[u] = [pairs[0][1], pairs[0][1] + 1]
            else:
                phys[u] = [min(idle, key=lambda b: (max(banks[b][0] + hop, st), (b + 1 in idle) + (b - 1 in idle), banks[b][0]))]
            for b in phys[u]:
                idle.remove(b)
            extra[j] = extra.get(j, []) + [y for b in phys[u] for y in banks[b][1]]
        start[j] = st
        free[x["eng"]] = st + x["cost"]
        fin[j] = st + x["cost"] + (0.0 if back else x["lat"])
        out.append(j)
        ready.remove(j)
        if not back:
            for u in x["units"]:
                todo[u] -= 1
                if todo[u] == 0:
                    for b in phys[u]:
                        banks[b] = (max(fin[y] for y in units[u]["nodes"]), units[u]["nodes"])
                        idle.append(b)
        for s in succ[j]:
            same = nodes[s]["eng"] == x["eng"] == "p"
            rdy[s] = max(rdy[s], fin[j] + (0.0 if same else hop))
            left[s] -= 1
            if left[s] == 0:
                ready.append(s)
    return {"end": max(fin), "start": start, "fin": fin, "order": out, "phys": phys, "extra": extra}


def search(nodes, units, cfg):
    n = len(nodes)
    for x in nodes:
        x["pre"], x["suc"] = sorted(x["deps"]), []
    for j, x in enumerate(nodes):
        for d in x["pre"]:
            nodes[d]["suc"].append(j)
    rng = np.random.RandomState(cfg["seed"])
    best, prio = None, [float(-j) for j in range(n)]
    for it in range(cfg["iters"]):
        b = place(nodes, units, cfg, prio, True)
        noise = rng.rand(n) * cfg["noise"] * (it > 0)
        f = place(nodes, units, cfg, [-b["fin"][j] + noise[j] - nodes[j]["early"] for j in range(n)])
        if f is not None and (best is None or f["end"] < best["end"]):
            best = f
        if best is not None:
            prio = [-y for y in (f or best)["fin"]]
    return best


def schedule(nodes, units, cfg):
    best = search(nodes, units, cfg)
    out, fin, start, phys = best["order"], best["fin"], best["start"], best["phys"]
    for j, e in best["extra"].items():
        nodes[j]["deps"] = nodes[j]["deps"] | set(e)
    cnt, known, clock, prog, nd, seen = {}, {}, {}, [], 0, {}
    for j in out:
        x = nodes[j]
        if x["kind"] == "x":
            x["sig"] = ("rx%d" % x["calls"], "rx")
            clock[j] = {}
            continue
        q = x["eng"]
        kn = known.setdefault(q, {})
        waits = {}
        for d in sorted(x["deps"], key=lambda y: -fin[y]):
            if nodes[d]["eng"] == q == "p":
                continue
            sem, val = nodes[d]["sig"]
            num = 1 if isinstance(val, str) else val
            if kn.get(sem, 0) < num:
                waits[sem] = val
                kn[sem] = num
                seen[sem] = max(seen.get(sem, 0), num)
                for k2, v2 in clock[d].items():
                    kn[k2] = max(kn.get(k2, 0), v2)
        if x["kind"] == "d":
            send = x["calls"][0][0] == "send"
            x["sig"] = ("d%d" % nd, "tx" if send else 16 * len(x["calls"]))
            nd += 1
        else:
            cnt[q] = cnt.get(q, 0) + len(x["calls"])
            x["sig"] = (q, cnt[q])
        clock[j] = dict(kn)
        prog.append((q, list(waits.items()), x["calls"], x["sig"][0], x["kind"]))
    last = {}
    for x in nodes:
        sem, val = x["sig"]
        num = 1 if isinstance(val, str) else val
        if seen.get(sem, 0) < num and (sem not in last or isinstance(val, str) or last[sem] < val):
            last[sem] = val
    return {"prog": prog, "phys": phys, "last": last, "end": max(fin), "start": start, "fin": fin, "nodes": nodes, "order": out}


_PLAN = {}


def plan():
    if "p" not in _PLAN:
        nodes, units = graph(CFG)
        _PLAN["p"] = schedule(nodes, units, CFG)
    return _PLAN["p"]


def routes(src, cores, topo):
    off = [c for c in cores if topo.chip(c) != topo.chip(src)]
    on = [c for c in cores if c != src and topo.chip(c) == topo.chip(src)]
    out, used = [], set()
    if off:
        eng = [e for e in topo.engines(src, off[0]) if all(e in topo.engines(src, c) for c in off)]
        used = set(eng)
        out.append((off, eng))
    if on:
        eng = [e for e in topo.engines(src, on[0]) if e not in used]
        out.append((on, eng[:CFG["on_eng"]]))
    return out


def rank_program(g, core, T, topo):
    rank = T.rank_of(core)
    if rank is None:
        return
    p = plan()
    cores = list(T.cores)
    mine = routes(core, cores, topo)
    tx = sum(len(e) for _, e in mine)
    rx = sum(len(e) for c in cores if c != core for to, e in routes(c, cores, topo) if core in to)
    Q = {"v": g.vector, "a": g.scalar, "p": g.tensor, "gq": g, "sync": g.sync}

    def ap(x):
        if not isinstance(x, tuple):
            return x
        if x[0] in "sh":
            return T[x[1]][x[2]]
        if x[0] == "i":
            return ap(x[1]).indirect(ap(x[2]))
        b = p["phys"][x[1]]
        if x[3] is not None:
            return T.PS[:, b[x[3]], x[2]]
        if len(b) == 1:
            return T.PS[:, b[0], x[2]]
        return T.PS[:, b[0]:b[1] + 1:b[1] - b[0], x[2]]

    def val(v):
        return {"rx": rx, "tx": tx}[v] if isinstance(v, str) else v

    def place(n, dst):
        d = (cores.index(dst) - rank) % NR - 1
        return T.WT[:, V + d * B:V + d * B + B] if n == 3 else T["land%d" % n][:, d, :]

    for q, waits, calls, sem, kind in p["prog"]:
        e = Q[q]
        for s, v in waits:
            e.wait_ge(T.sem[s], val(v))
        for c in calls:
            if c[0] == "send":
                trs = []
                for to, eng in mine:
                    ids = [DstId(rid=topo.addr(d)[0], pnc=topo.addr(d)[1]) for d in to]
                    trs.append(RemoteDMATransfer(dst_ids=ids, dma_engine_mask=sum(1 << x for x in eng), remote_sem=T.sem["rx%d" % c[1]],
                                                 srcs=[ap(c[2])], dsts=[place(c[1], d) for d in to]))
                g.remote_dma_fused(trs, local_sem=T.sem[sem])
                continue
            a = [ap(x) for x in c[1]]
            if c[0] == "tensor_scalar":
                ins = e.tensor_scalar(*a)
            elif c[0] == "tensor_tensor":
                ins = e.tensor_tensor(*a)
            elif c[0] == "tensor_copy":
                ins = e.tensor_copy(*a)
            elif c[0] == "memset":
                ins = e.memset(*a)
            elif c[0] == "activation":
                ins = e.activation(*a, bias=ap(c[2]["bias"]), scale=c[2]["scale"])
            elif c[0] == "matmul":
                ins = e.matmul(*a)
            elif c[0] == "iota":
                ins = e.iota(*a, **c[2])
            elif c[0] == "affine_select":
                ins = e.affine_select(*a)
            else:
                ins = e.dma_start(*a, **c[2])
            ins.then_inc(T.sem[sem], 16 if kind == "d" else 1)
    for s, v in p["last"].items():
        g.wait_ge(T.sem[s], val(v))
